import numpy as np, ml_dtypes
CORES = [48,51,52,55]
N = 4
import mx_ref
BF = ml_dtypes.bfloat16
def gentries(a):
    return np.ascontiguousarray(a.reshape(8, 16, -1).transpose(0, 2, 1)).reshape(8, -1)
def gtable(e):
    e = np.asarray(e); return np.ascontiguousarray(e.reshape(8, -1, 16).transpose(0, 2, 1)).reshape(128, -1).astype(np.int32)
def gcols(t, e):
    v = np.concatenate([t.reshape(8, 16, -1, 4), np.zeros((8, 16, 1, 4), BF)], axis=2)
    return np.ascontiguousarray(np.stack([v[g][:, e[g]] for g in range(8)])).reshape(128, -1)
def tile(rs):
    return np.stack(rs, axis=2).reshape(128, -1).astype(BF)
def cut(t, i, w=512):
    return t[:, w * i:w * i + w]
def pick(q, e):
    c = np.concatenate([q[0].reshape(128, -1, 4), np.zeros((128, 1, 4), np.uint8)], axis=1); s = np.concatenate([q[1], np.ones((16, 1), np.uint8)], axis=1)
    return (np.ascontiguousarray(c[:, e].reshape(128, -1)), np.ascontiguousarray(s[:, e]))
def join(*qs):
    return (np.concatenate([q[0] for q in qs], axis=1), np.concatenate([q[1] for q in qs], axis=1))
def put(q, e, v):
    c, s = q[0].reshape(128, -1, 4).copy(), q[1].copy(); c[:, e] = v[0].reshape(128, -1, 4); s[:, e] = v[1]
    return (c.reshape(128, -1), s)
def pk(c, s):
    return (np.ascontiguousarray(c), mx_ref.live(s))
def emit(q):
    return q[0], q[1]
def packed(v, rng):
    q = [mx_ref.quantize(np.ascontiguousarray(v[r])) for r in range(N)]
    return np.stack([a for a, b in q]), np.stack([mx_ref.plane(b, rng) for a, b in q])
def values_of_codes():
    e, c = np.zeros((128, 128, 4), np.float32), np.zeros((128, 2, 4), np.uint8)
    e[np.arange(128), np.arange(128), 0] = 1
    c[:127, :, 0] = np.arange(256).reshape(2, 128).T[:127]
    return mx_ref.matmul(mx_ref.quantize(e.reshape(128, 512).astype(BF)), (c.reshape(128, 8), np.full((16, 2), 127, np.uint8))).T.reshape(-1).astype(np.float64)
CODE_VALUE, SCALE_VALUE = values_of_codes(), 2.0 ** (np.arange(256) - 127.0)
def decode(q):
    return (CODE_VALUE[q[0]].reshape(16, 8, -1, 4) * SCALE_VALUE[q[1]][:, None, :, None] + 0.0).reshape(128, -1).astype(np.float32)
def f(rng, *shape):
    return mx_ref.flush((rng.standard_normal(shape, dtype=np.float32) * np.exp2(rng.integers(-2, 3, shape[:-1] + (1,)))).astype(BF))
def wide(rng, *shape, cols=0):
    v = rng.standard_normal(shape, dtype=np.float32) * np.exp2(rng.integers(-12, 13, shape)).astype(np.float32)
    if cols: v *= np.repeat(np.exp2(rng.integers(-cols, cols + 1, shape[:-2] + (1, shape[-1] // 4))) * (rng.random(shape[:-2] + (1, shape[-1] // 4)) > 0.0625), 4, axis=-1).astype(np.float32)
    return mx_ref.flush(v.astype(BF))
C, A, R = 384, 160, 3
STEP = [1, 2, 1]
def partner(r, t):
    return r ^ STEP[t]
def big(v, k):
    v = v.astype(np.float32) * np.float32(k)
    v[np.abs(v) < np.float32(2.0 ** -16)] = 0
    return v.astype(BF)
def common(w, rng):
    c, p = packed(np.stack([w] * N), rng)
    return {"wc": c, "ws": p}
def weights(rng, q=-1):
    w = big(f(rng, 128, 2048), 1).reshape(128, 4, 128, 4)
    if q >= 0:
        w[16 * q:16 * q + 8] = 0
        for i in range(16 * q, 16 * q + 8):
            w[:, :, i] = 0
            for b in range(4): w[i, b, i, b] = 64
    return common(w.reshape(128, 2048), rng)
def numbers_of(rng):
    return {"x": big(f(rng, N, 128, 4 * C), 1), "u": np.array(f(rng, N, 128, 512)), "v": np.array(f(rng, N, 128, 512))}
def lists_of(rng):
    return {"m": np.argsort(rng.random((N, 8, C)), axis=2), "la": rng.integers(0, C, (N, 8, R * A)), "lb": rng.integers(0, C, (N, 8, R * A)),
            "ld": np.argsort(rng.random((N, 8, R, C)), axis=3)[:, :, :, :A].reshape(N, 8, R * A)}
def stored(l):
    return {k: np.stack([gtable(e) for e in l[k]]) for k in ("m", "la", "lb", "ld")}
def setup_inputs(rng):
    return {**numbers_of(rng), **stored(lists_of(rng)), **weights(rng)}
def setup_inputs_rolls(rng):
    d, l = numbers_of(rng), lists_of(rng)
    q = int(rng.integers(8))
    o = rng.permutation(N)
    back = []
    for r in range(N):
        g = rng.permutation(8)
        if o[r] % 3 == 2: g = rng.permutation(7)
        while abs(int(g[0]) - int(g[1])) < 2: g = np.roll(g, 1)
        back.append([[(0, 1), (1, 2), (2, 3)], [(0, 1), (2, 3), (0, 2)], [(0, 1), (0, 1), (0, 1)]][o[r] % 3])
        back[r] = [[int(g[i]) for i in e] for e in back[r]]
    size = np.exp2(np.array([-30.0, -12.0, 0.0, 10.0])[rng.permutation(N) % 4]).astype(np.float32)
    mark = np.zeros((27, 8, 4), np.float32)
    for k in range(9):
        for i in range(2):
            mark[k + 9 * i, :, 0] = i
            if k < 8: mark[k + 9 * i, k] = (0, 2, 0, 0)
        mark[18 + k, :, 1] = 2
        if k < 8: mark[18 + k, k] = 0
    x = d["x"].reshape(N, 8, 16, C, 4)
    u = d["u"].reshape(N, 128, 128, 4)
    u[:, :, ::16] = 0
    one = np.ones(N, np.float32)
    for r in range(N):
        if size[r] < 2.0 ** -20:
            for t in range(R): one[partner(r, t)] = 2.0 ** -30
    for g in range(8):
        u[:, 16 * q + g, 16 * g, 0] = one.astype(BF)
        u[:, 16 * q + g, 16 * g, 1] = (-one).astype(BF)
    for r in range(N):
        e = rng.permutation(C)
        written, pool = e[:A], e[A:]
        kind = rng.integers(0, 27, C)
        kind[l["m"][r, q, pool]] = np.arange(C - A) % 27
        x[r, q, :8] = (mark[kind].transpose(1, 0, 2) * size[r]).astype(BF)
        for t in range(R):
            l["ld"][r, q, A * t:A * t + A] = rng.permutation(written)
            p = back[partner(r, t)][t]
            most = o[partner(r, t)] == 2 and t == R - 1
            h = A - 1 if most else int(rng.integers(2, A // 4))
            n = np.full(8, h - 1)
            if (o[partner(r, t)] + t) % 2 == 0:
                n[min(p):] = h
                n[max(p)] = h + 1
            else:
                n[p] = h
                n[max(p) + 1:] = h
            k = np.full(2 * A, 8)
            if most: k[:A] = 26
            s = np.repeat(18 + np.arange(8), A - n) if most else np.repeat(np.arange(8), n)
            k[:len(s)] = s
            e = pool[k + 9 * rng.integers(0, 2, 2 * A) * (k < 9) + 27 * rng.integers(0, (C - A) // 27, 2 * A)]
            j = rng.permutation(A)
            l["la"][r, q, A * t:A * t + A] = e[:A][j]
            l["lb"][r, q, A * t:A * t + A] = e[A:][j]
    return {"x": x.reshape(N, 128, 4 * C), "u": u.reshape(N, 128, 512), "v": d["v"], **stored(l), **weights(rng, q)}
def setup_inputs_lists(rng):
    d, l = numbers_of(rng), lists_of(rng)
    o = rng.permutation(N)
    for r in range(N):
        if o[r] == 2:
            l["m"][r] = rng.permutation(C)[None, :]
            e = l["m"][r, 0, C - 8:]
            x = np.zeros((128, C, 4), BF)
            x[:, e] = d["x"][r].reshape(128, C, 4)[:, e]
            d["x"][r] = x.reshape(128, 4 * C)
            l["la"][r] %= C - 8
            l["lb"][r] %= C - 8
            l["ld"][r] = np.argsort(rng.random((8, R, C - 8)), axis=2)[:, :, :A].reshape(8, R * A)
        elif o[r] % 2:
            e = np.repeat(l["ld"][r, :, :1], R * A, axis=1)
            l["la"][r] = e
            l["lb"][r] = e
        else:
            e = l["ld"][r, :, :A].copy()
            l["ld"][r] = np.tile(e, (1, R))
            l["la"][r] = np.tile(e, (1, R))
            l["lb"][r] = np.tile(e[:, ::-1], (1, R))
    return {**d, **stored(l), **weights(rng)}
def setup_inputs_huge(rng):
    d, l = numbers_of(rng), lists_of(rng)
    o = rng.permutation(N)
    g = np.ones((N, 8))
    for r in range(N):
        if o[r] == 0: g[r] = -1
        if o[r] == 2: g[r, 0] = -1
        if o[r] > 2: g[r] = rng.permutation(8) % 2 * 2.0 - 1.0
    x = 2.0 ** 28 * (1.5 + 0.5 * rng.random((N, 128, 4 * C)))
    u = d["u"].reshape(N, 128, 128, 4)
    u[:, :, ::16] = (2.0 ** 30 * (0.75 + 0.25 * rng.random((N, 128, 8, 4))) * g[:, None, :, None]).astype(np.float32).astype(BF)
    w = np.zeros((128, 4, 128, 4), np.float32)
    i = np.arange(128)
    for b in range(4): w[i, b, i, b] = 32
    return {"x": x.astype(np.float32).astype(BF), "u": u.reshape(N, 128, 512), "v": d["v"], **stored(l), **common(w.reshape(128, 2048).astype(BF), rng)}
def setup_inputs_spread(rng):
    d = setup_inputs(rng)
    d["x"] = big(wide(rng, N, 128, 4 * C, cols=6), 1)
    return d
def check_inputs(d):
    b = []
    for k in ("x", "u", "v"):
        a = np.abs(d[k].astype(np.float32))
        if not (np.isfinite(a).all() and ((a == 0) | (a >= 2.0 ** -30) & (a <= 2.0 ** 30)).all()): b.append("a value of " + k)
    for r in range(N):
        if (np.sort(gentries(d["m"][r]), axis=1) != np.arange(C)).any(): b.append("m: a group's entries aren't a permutation")
        for k in ("la", "lb", "ld"):
            if ((d[k][r] < 0) | (d[k][r] >= C)).any(): b.append("an entry of " + k)
        s = np.sort(gentries(d["ld"][r]).reshape(8, R, A), axis=2)
        if (s[:, :, 1:] == s[:, :, :-1]).any(): b.append("ld: equal entries of a group in a round")
    if (d["wc"] != d["wc"][:1]).any(): b.append("wc differs between ranks")
    s = [mx_ref.live(p) for p in d["ws"]]
    if any((p != s[0]).any() for p in s): b.append("ws differs between ranks")
    return b
def reference(x, u, v, m, la, lb, ld, wc, ws):
    w = pk(wc[0], ws[0])
    qu = [mx_ref.quantize(u[r]) for r in range(N)]
    kept = [x[r] for r in range(N)]
    maps = [[gentries(m[r]).astype(np.int64)] for r in range(N)]
    for t in range(R):
        sent = []
        for r in range(N):
            now = maps[r][t]
            one = gcols(kept[r], np.take_along_axis(now, gentries(la[r])[:, A * t:A * t + A], axis=1))
            two = gcols(kept[r], np.take_along_axis(now, gentries(lb[r])[:, A * t:A * t + A], axis=1))
            q = mx_ref.quantize((one.astype(np.float32) + two.astype(np.float32)).astype(BF))
            h = tile([np.maximum(mx_ref.matmul(pick(w, np.arange(128 * b, 128 * b + 128)), q), np.float32(0.0)) * np.float32(0.015625) for b in range(4)])
            sent.append(mx_ref.quantize(h))
        came = decode(join(*sent)).astype(BF)
        for r in range(N):
            e = partner(r, t)
            yes = mx_ref.matmul(qu[r], sent[e])[::16] + np.float32(0.0) >= 0
            kept[r] = np.concatenate([kept[r], cut(came, e, 4 * A)], axis=1)
            to = gentries(ld[r])[:, A * t:A * t + A]
            new = maps[r][t].copy()
            for g in range(8): new[g, to[g][yes[g]]] = C + A * t + np.flatnonzero(yes[g])
            n = np.sum(~yes, axis=1)
            for g in np.argsort(-n, kind="stable")[:2]: new[g] = maps[r][max(t - 1, 0)][g]
            maps[r].append(new)
    y, om = np.zeros((N, 128, C), np.float32), np.zeros((N, 8, C), np.float32)
    oc, osc = np.zeros((N, 128, 4 * C), np.uint8), np.zeros((N, 16, C), np.uint8)
    for r in range(N):
        q = mx_ref.quantize(gcols(kept[r], maps[r][R]))
        y[r] = mx_ref.matmul(mx_ref.quantize(v[r]), q)
        om[r] = maps[r][R]
        oc[r], osc[r] = emit(q)
    return {"y": y, "om": om, "oc": oc, "osc": osc}

@@ -1,0 +1,432 @@
+from concourse.mybir import dt, AluOpType, ActivationFunctionType
+
+C, A, R = 384, 160, 3
+STEP = [1, 2, 1]
+HALF = "float16"
+
+
+def _sb(n, d="float32"):
+    return ("sbuf", [128, n], d)
+
+
+SCRATCH = {
+    "lst": _sb(128, "int32"), "lu": _sb(128, "uint16"),
+    "F": _sb(4 * (C + R * A), "bfloat16"), "ut": _sb(512, "bfloat16"), "vt": _sb(512, "bfloat16"),
+    "wq": _sb(512, "float8_e4m3fn_x4"), "wp": _sb(512, "uint8"),
+    "uq": _sb(128, "float8_e4m3fn_x4"), "up": _sb(128, "uint8"),
+    "u2q": _sb(256, "float8_e4m3fn_x4"), "u2p": _sb(256, "uint8"),
+    "vq": _sb(128, "float8_e4m3fn_x4"), "vp": _sb(128, "uint8"),
+    "eb": _sb(520, "bfloat16"), "eq": _sb(512, "float8_e4m3fn_x4"), "ep": _sb(512, "uint8"),
+    "ramp": _sb(C + R * A), "pi": _sb(8, "int32"), "pf": _sb(8), "cf": _sb(8),
+    "em4": _sb(A), "mask4": _sb(A), "u2i": _sb(8, "int32"), "u2j": _sb(8, "int32"),
+    "RL": _sb(24, "uint16"), "UL": _sb(16, "uint16"), "OL": _sb(2, "uint16"),
+    "b0": _sb(32), "b1": _sb(32), "c8": _sb(8),
+    "d0n": _sb(C, "bfloat16"), "d0h": _sb(2 * C, "bfloat16"),
+    "P": _sb(2 * C, HALF), "XO": _sb(2 * C, HALF), "Pn": _sb(2 * A, HALF), "Xn": _sb(2 * A, HALF),
+    "M0": _sb(C), "C0": _sb(C), "C1": _sb(C), "m0s": _sb(96), "inv": _sb(C), "krep": _sb(C), "Pk": _sb(C),
+    "rbg": _sb(C), "odg": _sb(C), "Xs": _sb(C), "rbs": _sb(96),
+    "O": _sb(96, "uint16"), "fw": _sb(176), "fk": _sb(A), "wk": _sb(A),
+    "sg": _sb(A), "key": _sb(2), "bc": _sb(32), "tr": _sb(32), "cm": _sb(8), "r8": _sb(8),
+    "Bt": _sb(4 * A, "bfloat16"), "Z": _sb(4 * A, "bfloat16"), "H": _sb(4 * A, "bfloat16"),
+    "hq": _sb(A, "float8_e4m3fn_x4"), "hp": _sb(A, "uint8"),
+    "Tt": _sb(4 * C, "bfloat16"), "tq": _sb(C, "float8_e4m3fn_x4"), "tp": _sb(C, "uint8"),
+    "ys": _sb(C), "Rr": _sb(128), "Rt": _sb(128), "omc": _sb(32),
+}
+for _t in range(R):
+    SCRATCH["zq%d" % _t] = _sb(A, "float8_e4m3fn_x4")
+    SCRATCH["zp%d" % _t] = _sb(A, "uint8")
+    SCRATCH["gq%d" % _t] = _sb(A, "float8_e4m3fn_x4")
+    SCRATCH["gp%d" % _t] = _sb(A, "uint8")
+    SCRATCH["ro%d" % _t] = _sb(C)
+    SCRATCH["kl%d" % _t] = _sb(24)
+    SCRATCH["KO%d" % _t] = _sb(24, "uint16")
+for _b in range(8):
+    SCRATCH["ps%d" % _b] = ("psum", [128, 512], "float32")
+
+SEMAPHORES = ["cV", "cA", "cT", "cG", "sent", "outs", "arr0", "arr1", "arr2",
+              "dm", "dla", "dlb", "dld", "dx", "du", "dv", "dwc", "dws", "dk0", "dk1", "dk2"]
+
+ALU = AluOpType
+ACT = ActivationFunctionType
+
+
+def emit(g, T, ops):
+    queue = {"V": g.vector, "A": g.scalar, "T": g.tensor, "G": g, "S": g.sync}
+    writer, readers, clock, seq = {}, {}, {q: {} for q in queue}, {q: 0 for q in queue}
+    for i, o in enumerate(ops):
+        deps = set()
+        for k in o["r"]:
+            deps.add(writer[k])
+        for k in o["w"]:
+            if k in writer:
+                deps.add(writer[k])
+            deps.update(readers.get(k, []))
+        deps.discard(i)
+        o["waits"] = []
+        if o["q"] is None:
+            o["knows"] = {}
+        else:
+            known = clock[o["q"]]
+            for d in sorted(deps, reverse=True):
+                p = ops[d]
+                if known.get(p["lane"], -1) >= p["pos"]:
+                    continue
+                if p["q"] == "T" and o["q"] == "T":
+                    continue
+                o["waits"].append(d)
+                p["signal"] = True
+                for lane, pos in p["knows"].items():
+                    known[lane] = max(known.get(lane, -1), pos)
+            o["knows"] = dict(known)
+        if o["sem"] is None:
+            o["lane"], o["pos"] = o["q"], seq[o["q"]]
+            seq[o["q"]] += 1
+        else:
+            o["lane"], o["pos"] = ("dma", i), 0
+        o["knows"][o["lane"]] = o["pos"]
+        for k in o["r"]:
+            readers.setdefault(k, []).append(i)
+        for k in o["w"]:
+            writer[k] = i
+            readers[k] = []
+    count = {}
+    for o in ops:
+        if o["sem"] is not None:
+            count[o["sem"]] = count.get(o["sem"], 0) + o["inc"]
+            o["at"] = (o["sem"], count[o["sem"]])
+        elif o.get("signal"):
+            name = "c" + o["q"]
+            count[name] = count.get(name, 0) + 1
+            o["at"] = (name, count[name])
+    for o in ops:
+        if o["q"] is None:
+            continue
+        for d in o["waits"]:
+            queue[o["q"]].wait_ge(T.sem[ops[d]["at"][0]], ops[d]["at"][1])
+        call = o["fn"]()
+        if o["sem"] is None:
+            if o.get("signal"):
+                call.then_inc(T.sem[o["at"][0]], 1)
+        elif o["local"]:
+            call.then_inc(T.sem[o["sem"]], 16)
+    return count
+
+
+def rank_program(g, core, T, topo):
+    rank = T.rank_of(core)
+    if rank is None:
+        return
+    ops = []
+    V, S, PE = g.vector, g.scalar, g.tensor
+
+    def op(q, fn, r, w):
+        ops.append({"q": q, "fn": fn, "r": list(r), "w": list(w), "sem": None})
+
+    def dma(q, sem, out, in_, r, w):
+        eng = {"A": g.scalar, "S": g.sync, "G": g}[q]
+        ops.append({"q": q, "fn": lambda: eng.dma_start(out, in_), "r": list(r), "w": list(w), "sem": sem, "inc": 16, "local": True})
+
+    def ts(out, in0, s1, s2, op0, op1, r, w):
+        if op1 is None:
+            op("V", lambda: V.tensor_scalar(out, in0, s1, None, op0), r, w)
+        else:
+            op("V", lambda: V.tensor_scalar(out, in0, s1, s2, op0, op1), r, w)
+
+    def tt(out, in0, in1, alu, r, w):
+        op("V", lambda: V.tensor_tensor(out, in0, in1, alu), r, w)
+
+    def cp(out, in_, r, w):
+        op("V", lambda: V.tensor_copy(out, in_), r, w)
+
+    def fill(ap, c, w):
+        op("V", lambda: V.memset(ap, c), [], w)
+
+    def scan(out, d0, d1, init, op0, op1, r, w):
+        op("V", lambda: V.tensor_tensor_scan(out, d0, d1, init, op0, op1), r, w)
+
+    def quant(q, s, t, r, w):
+        op("V", lambda: V.quantize_mx(q, s, t), r, w)
+
+    def act(out, in_, func, r, w, **kw):
+        op("A", lambda: S.activation(out, in_, func, **kw), r, w)
+
+    def afill(out, c, w):
+        n = out.shape[1]
+        act(out, T.ramp[:, 0:n], ACT.Identity, ["ramp"], w, scale=0.0, bias=float(c))
+
+    def mm(bank, n, lq, lp, rq, rp, r):
+        op("T", lambda: PE.matmul_mx(T["ps%d" % bank][:, 0:n], lq, lp, rq, rp, True, True), r, ["ps%d" % bank])
+
+    def iota(out, pattern, base, cm, w, whole=False):
+        if whole:
+            op("G", lambda: g.iota(out, pattern, base, cm), [], w)
+        else:
+            op("G", lambda: g.iota(out, pattern, base, cm, allow_small_or_imprecise_dtypes=True), [], w)
+
+    def mask_by_quarter(out, in_, n, r, w):
+        for q in range(4):
+            act(out[:, q:n:4], in_[:, q:n:4], ACT.Copy, r + ["mask4"], [k + str(q) for k in w], scale=T.mask4[:, q:q + 1])
+
+    quarters = lambda k: [k + str(q) for q in range(4)]
+    LM, LA, LB, LD = 0, 24, 54, 84
+    la = lambda t: T.lu[:, LA + 10 * t:LA + 10 * t + 10]
+    lb = lambda t: T.lu[:, LB + 10 * t:LB + 10 * t + 10]
+    ld = lambda t: T.lu[:, LD + 10 * t:LD + 10 * t + 10]
+    M0 = T.M0[:]
+    tcol, qcol = T.pf[:, 1:2], T.pf[:, 2:3]
+    file_keys = lambda t: ["x"] + ["F%d%d" % (s, b) for s in range(t) for b in range(4)]
+    window = lambda t: T.F[:, 0:4 * (C + A * t)]
+
+    dma("S", "dm", T.lst[:, LM:LM + 24], T.m[:], [], ["m"])
+    dma("A", "dlb", T.lst[:, LB:LB + 30], T.lb[:], [], ["lb"])
+    dma("S", "dla", T.lst[:, LA:LA + 30], T.la[:], [], ["la"])
+    dma("S", "dx", T.F[:, 0:4 * C], T.x[:], [], ["x"])
+    dma("S", "dld", T.lst[:, LD:LD + 30], T.ld[:], [], ["ld"])
+    dma("S", "du", T.ut[:], T.u[:], ["m"], ["ut"])
+    dma("S", "dws", T.wp[:], T.ws[:], [], ["wp"])
+    dma("S", "dwc", T.wq[:].bitcast(dt.uint8), T.wc[:], [], ["wq"])
+    dma("S", "dv", T.vt[:], T.v[:], [], ["vt"])
+
+    iota(T.pi[:, 0:1], [[0, 1]], 0, 1, ["pi0"], True)
+    iota(T.em4[:], [[0, 40], [1, 4]], 0, 0, ["em4"])
+    iota(T.ramp[:, 0:C], [[1, C]], 0, 0, ["ramp"])
+    iota(T.u2i[:], [[2, 4], [0, 2]], 0, 1, ["u2i"], True)
+    fill(T.d0h[:], 1.0, ["d0h", "keep"])
+    iota(T.ramp[:, C:C + R * A], [[1, R * A]], C, 0, ["ramp2"])
+    op("G", lambda: g.affine_select(T.eb[:, 0:516], T.d0h[:, 0:516], [[-1, 516]], ALU.is_equal, 0.0, 3, 4), ["d0h", "keep"], ["eb"])
+    fill(T.d0n[:], 1.0, ["d0n"])
+    p0 = T.pi[:, 0:1]
+    ts(T.pi[:, 1:2], p0, 3, None, ALU.bitwise_and, None, ["pi0"], ["pi1"])
+    ts(T.pi[:, 2:3], p0, 2, 3, ALU.logical_shift_right, ALU.bitwise_and, ["pi0"], ["pi2"])
+    ts(T.pi[:, 5:6], p0, 4, 6, ALU.logical_shift_right, ALU.bitwise_and, ["pi0"], ["pi5"])
+    ts(T.pi[:, 3:4], p0, 15, None, ALU.bitwise_and, None, ["pi0"], ["pi3"])
+    ts(T.pi[:, 4:5], p0, 31, None, ALU.bitwise_and, None, ["pi0"], ["pi4"])
+    tt(T.pi[:, 6:7], p0, T.pi[:, 5:6], ALU.add, ["pi0", "pi5"], ["pi6"])
+    fill(T.d0n[:, 0:C:4], 0.0, ["d0n"])
+    ts(T.pi[:, 7:8], T.pi[:, 6:7], 7, None, ALU.bitwise_and, None, ["pi6"], ["pi7"])
+    fill(T.inv[:], 0.0, ["inv"])
+    cp(T.pf[:], T.pi[:], ["pi%d" % i for i in range(8)], ["pf"])
+    ts(T.P[:, 1:2 * C:2], T.d0n[:], 0.0, None, ALU.mult, None, ["d0n"], ["h0", "h1", "h2", "h3"])
+    ts(T.mask4[:], T.em4[:], qcol, None, ALU.is_equal, None, ["em4", "pf"], ["mask4"])
+    act(T.cf[:, 1:2], T.pf[:, 3:4], ACT.Identity, ["pf"], ["cf1"], scale=16.0)
+    ts(T.u2j[:], T.u2i[:], 7, None, ALU.bitwise_and, None, ["u2i"], ["u2j"])
+    ts(T.UL[:, 0:8], T.ramp[:, 0:8], 16.0, None, ALU.mult, None, ["ramp"], ["ULa"])
+    ts(T.UL[:, 8:16], T.u2j[:], 16.0, None, ALU.mult, None, ["u2j"], ["ULb"])
+    ts(T.cf[:, 2:3], T.pf[:, 3:4], 8.0, float(1 - C), ALU.is_ge, ALU.mult, ["pf"], ["cf2"])
+    ts(T.RL[:, 0:24:3], T.ramp[:, 0:16:2], T.cf[:, 1:2], None, ALU.add, None, ["ramp", "cf1"], ["RL0"])
+    ts(T.RL[:, 2:24:3], T.ramp[:, 129:145:2], T.cf[:, 1:2], None, ALU.add, None, ["ramp", "cf1"], ["RL2"])
+    ts(T.RL[:, 1:24:3], T.ramp[:, 256:272:2], T.cf[:, 1:2], T.cf[:, 2:3], ALU.add, ALU.add, ["ramp", "cf1", "cf2"], ["RL1"])
+    act(T.cf[:, 3:4], qcol, ACT.Identity, ["pf"], ["cf3"], scale=8.0, bias=tcol)
+    act(T.cf[:, 4:5], T.pf[:, 7:8], ACT.Identity, ["pf"], ["cf4"], scale=-0.125, bias=A / 2 + 0.875)
+    afill(T.b0[:], 1, ["b0", "b0a", "b0b"])
+    afill(T.b1[:], 0, ["b1"])
+    afill(T.fw[:, 0:1], 0, ["fw0"])
+    afill(T.krep[:, 2 * A:C], 0, ["krept"])
+    afill(T.Rr[:, 96:128], 0, ["Rrt"])
+    afill(T.c8[:, 0:7], -100, ["c8a"])
+    afill(T.c8[:, 7:8], 0, ["c8b"])
+
+    def offsets(src, lo, n, r, w):
+        ts(T.O[:, lo:lo + n], src, 4.0, tcol, ALU.mult, ALU.add, r + ["pf"], [w])
+
+    def engine_sets(t, src, dst):
+        e = topo.engines(src, dst)
+        return (e[:len(e) // 2], e[len(e) // 2:]) if t == 0 else (e, e)
+
+    def operands_and_send(t):
+        keys = file_keys(t)
+        for i in range(4):
+            act(T.Bt[:, A * i:A * i + A], window(t).indirect(T.O[:, 10 * i:10 * i + 10]), ACT.Copy, keys + ["O0"], ["Bt%d" % i])
+        for i in range(4):
+            tt(T.Z[:, A * i:A * i + A], window(t).indirect(T.O[:, 40 + 10 * i:50 + 10 * i]), T.Bt[:, A * i:A * i + A], ALU.add,
+               keys + ["O1", "Bt%d" % i], ["Z%d" % i])
+        quant(T["zq%d" % t][:], T["zp%d" % t][:], T.Z[:], quarters("Z"), ["zq%d" % t])
+        peer = T.cores[rank ^ STEP[t]]
+        rid, pid = topo.addr(peer)[0:2]
+        sides = ((T["gq%d" % t][:].bitcast(dt.uint8), T["zq%d" % t][:].bitcast(dt.uint8)), (T["gp%d" % t][:], T["zp%d" % t][:]))
+        for (out, in_), es in zip(sides, engine_sets(t, core, peer)):
+            mask = sum(1 << e for e in es)
+            ops.append({"q": "G", "r": ["zq%d" % t], "w": [], "sem": "sent", "inc": len(es), "local": False,
+                        "fn": lambda out=out, in_=in_, mask=mask: g.remote_dma(out, in_, T.sem["arr%d" % t], T.sem.sent, pid, rid, mask)})
+        ops.append({"q": None, "r": [], "w": ["gq%d" % t], "sem": "arr%d" % t, "inc": sum(len(es) for es in engine_sets(t, peer, core))})
+
+    def renamers(t):
+        lo = C + A * t
+        cp(T.inv[:].indirect(ld(t)), T.ramp[:, lo:lo + A], ["ramp2", "ldu"], ["inv"])
+
+    def renamers_of_operands(t):
+        act(T.krep[:, 0:A], T.inv[:].indirect(lb(t)), ACT.Copy, ["inv", "lbu"], ["krepb"])
+        act(T.krep[:, A:2 * A], T.inv[:].indirect(la(t)), ACT.Copy, ["inv", "lau"], ["krepa"])
+
+    def to_list(t, src, r, after):
+        act(T["ro%d" % t][:], src.indirect(T.RL[:]), ACT.Copy, r + ["RL0", "RL1", "RL2"], ["ro%d" % t])
+        dma("S", "dk%d" % t, T["kl%d" % t][:], T["ro%d" % t][0:128:16, :], ["ro%d" % t] + after, ["kl%d" % t])
+
+    def slots(src, n, r):
+        scan(T.Xs[:, 0:n], T.d0n[:, 0:n], src[:, 0:n], 0.0, ALU.mult, ALU.add, r + ["d0n"], ["Xs"])
+
+    def commit(t):
+        lo = C + A * t
+        tt(T.wk[:], T.fk[:], T.ramp[:, lo:lo + A], ALU.min, ["fk", "ramp2"], ["wk"])
+        cp(T["C%d" % t][:].indirect(ld(t)), T.wk[:], ["wk", "ldu"], ["C%d" % t])
+
+    def kept_flags():
+        act(T.fk[:], T.fw[:, 1:A + 1], ACT.Copy, ["fw", "r8"], ["fk"], scale=T.r8[:, 7:8])
+
+    def after_arrival(t):
+        gq, gp, n = T["gq%d" % t][:], T["gp%d" % t][:], (C if t == R - 1 else 2 * A)
+        h = n // 2
+        for b in range(4):
+            mm(b, A, T.wq[:, 128 * b:128 * b + 128], T.wp[:, 128 * b:128 * b + 128], gq, gp, ["wq", "wp", "gq%d" % t])
+        for b in range(4):
+            bank = T["ps%d" % b][:, 0:A]
+            if b % 2 == 1:
+                ts(T.H[:, b:4 * A:4], bank, 0.0, 0.015625, ALU.max, ALU.mult, [], ["H%d" % b, "ps%d" % b])
+            else:
+                act(T.H[:, b:4 * A:4], bank, ACT.Relu, [], ["H%d" % b, "ps%d" % b], scale=0.015625)
+        quant(T.hq[:], T.hp[:], T.H[:], quarters("H"), ["hq"])
+        mm(5, A, T.u2q[:, 128:256], T.u2p[:, 128:256], T.hq[:], T.hp[:], ["u2q", "u2p", "hq"])
+        mm(4, A, T.u2q[:, 0:128], T.u2p[:, 0:128], T.hq[:], T.hp[:], ["u2q", "u2p", "hq"])
+        for b in range(4):
+            mm(b, A, T.eq[:, 128 * b:128 * b + 128], T.ep[:, 128 * b:128 * b + 128], T.hq[:], T.hp[:], ["eq%d" % b, "hq"])
+        KO = T["KO%d" % t]
+        ts(KO[:, 0:n // 16], T["kl%d" % t][:, 0:n // 16], float(1 - C - A * t), 0.0, ALU.add, ALU.max, ["kl%d" % t], ["KO"])
+        act(T.sg[:], T.ps5[:, 0:A], ACT.Sign, [], ["key", "ps5"], scale=2.0 ** 32, bias=2.0 ** -120, accum_out=T.key[:, 0:1])
+        lo = 4 * (C + A * t)
+        for b in range(4):
+            act(T.F[:, lo + b:lo + 4 * A:4], T["ps%d" % b][:, 0:A], ACT.Copy, [], ["F%d%d" % (t, b), "ps%d" % b])
+        ts(T.fw[:, 1:A + 1], T.ps4[:, 0:A], 0.0, 1024.0, ALU.is_ge, ALU.mult, [], ["fw", "ps4"])
+        cuts = [0, 4 if n < C else 6, n // 32, n // 32 + 6, n // 16]
+
+        def flags(i):
+            a, b = cuts[i], cuts[i + 1]
+            tt(T.P[:, 32 * a:32 * b:2], T.fw[:, 0:A + 1].indirect(KO[:, a:b]), T.Pk[:, 16 * a:16 * b],
+               ALU.min, ["fw", "fw0", "KO"] + quarters("Pk"), ["f%d" % i])
+        scan(T.bc[:], T.b0[:], T.b1[:], T.key[:, 0:1], ALU.mult, ALU.add, ["b0", "b0a", "b0b", "b1", "key"], ["bc"])
+        flags(0)
+        op("V", lambda: V.transpose(T.tr[:], T.bc[:]), ["bc"], ["tr"])
+        flags(1)
+        ts(T.cm[:], T.tr[:, 0:8], T.tr[:, 8:9], T.tr[:, 9:10], ALU.subtract, ALU.is_gt, ["tr"], ["cm"])
+        flags(2)
+        scan(T.r8[:], T.cm[:], T.c8[:], -1.0, ALU.add, ALU.max, ["cm", "c8a", "c8b"], ["r8"])
+        flags(3)
+        ts(T.d0h[:, 7:2 * n:8], T.d0n[:, 1:n:4], T.r8[:, 7:8], None, ALU.min, None, ["d0n", "r8"], ["keep"])
+        if t == R - 1:
+            ts(T.P[:, 7:2 * n:8], T.rbs[:], T.r8[:, 7:8], 1024.0, ALU.subtract, ALU.mult, ["rbs", "r8"], ["h3"])
+        for i in range(2):
+            a, b = 2 * h * i, 2 * h * (i + 1)
+            scan(T.XO[:, a:b], T.d0h[:, a:b], T.P[:, a:b], 0.0, ALU.mult, ALU.max,
+                 ["d0h", "keep", "h0", "h1", "h2", "h3", "f%d" % (2 * i), "f%d" % (2 * i + 1)], ["XO%d" % i])
+            offsets(T.XO[:, a + 7:b:8], i * h // 4, h // 4, ["XO%d" % i], "O%d" % i)
+
+    cp(T.lu[:, LM:LM + 24], T.lst[:, LM:LM + 24], ["m"], ["mu"])
+    cp(T.M0[:, 0:192], T.ramp[:, 0:C].indirect(T.lu[:, 0:12]), ["ramp", "mu"], ["M0a"])
+    act(T.M0[:, 192:C], T.ramp[:, 0:C].indirect(T.lu[:, 12:24]), ACT.Copy, ["ramp", "mu"], ["M0b"])
+    for i, (lo, l, key) in enumerate(((LB, lb(0), "lb"), (LA, la(0), "la"))):
+        cp(T.lu[:, lo:lo + 30], T.lst[:, lo:lo + 30], [key], [key + "u"])
+        tt(T.Pn[:, A * i:A * i + A], M0.indirect(l), T.mask4[:], ALU.mult, ["M0a", "M0b", key + "u", "mask4"], ["Pn%d" % i])
+        scan(T.Xn[:, A * i:A * i + A], T.d0n[:, 0:A], T.Pn[:, A * i:A * i + A], 0.0, ALU.mult, ALU.add, ["d0n", "Pn%d" % i], ["Xn%d" % i])
+        offsets(T.Xn[:, A * i + 3:A * i + A:4], 40 * i, 40, ["Xn%d" % i], "O%d" % i)
+    act(T.rbg[:, 0:A], M0.indirect(lb(1)), ACT.Copy, ["M0a", "M0b", "lbu"], quarters("rbb"))
+    operands_and_send(0)
+
+    RB = quarters("rba") + quarters("rbb")
+    iota(T.C0[:], [[0, C]], 0, 0, ["C0"])
+    iota(T.C1[:], [[0, C]], 0, 0, ["C1"])
+    cp(T.lu[:, LD:LD + 30], T.lst[:, LD:LD + 30], ["ld"], ["ldu"])
+    renamers(0)
+    act(T.rbg[:, A:2 * A], M0.indirect(la(1)), ACT.Copy, ["M0a", "M0b", "lau"], quarters("rba"))
+    mask_by_quarter(T.rbg, T.rbg, 2 * A, [], ["rba", "rbb"])
+    renamers_of_operands(1)
+    to_list(0, T.krep[:], ["krepa", "krepb", "krept"], [])
+    quant(T.uq[:], T.up[:], T.ut[:], ["ut"], ["uq"])
+    fill(T.d0h[:, 0:2 * C:8], 0.0, ["d0h"])
+    cp(T.u2q[:].bitcast(dt.uint32), T.uq[:].bitcast(dt.uint32).indirect(T.UL[:]), ["uq", "ULa", "ULb"], ["u2q"])
+    act(T.u2p[:], T.up[:].indirect(T.UL[:]), ACT.Copy, ["uq", "ULa", "ULb"], ["u2p"])
+    mask_by_quarter(T.Pk, T.krep, 2 * A, ["krepa", "krepb"], ["Pk"])
+    slots(T.rbg, 2 * A, RB)
+    ts(T.cf[:, 5:6], T.pf[:, 4:5], 9.0, 4095.0, ALU.is_equal, ALU.mult, ["pf"], ["cf5"])
+    cp(T.P[:, 7:4 * A:8], T.Xs[:, 3:2 * A:4], ["Xs"], ["h3"])
+    ts(T.b0[:, 16:17], T.pf[:, 4:5], 8.0, T.cf[:, 5:6], ALU.not_equal, ALU.add, ["pf", "cf5"], ["b0b"])
+    ts(T.b0[:, 0:1], T.cf[:, 5:6], -4096.0, 1.0 / 8192, ALU.add, ALU.mult, ["cf5"], ["b0a"])
+    renamers(1)
+    ts(T.b1[:, 0:1], T.cf[:, 4:5], T.b0[:, 0:1], -2.0, ALU.mult, ALU.mult, ["cf4", "b0a"], ["b1"])
+    for b in range(4):
+        quant(T.eq[:, 128 * b:128 * b + 128], T.ep[:, 128 * b:128 * b + 128], T.eb[:, 3 - b:515 - b], ["eb"], ["eq%d" % b])
+    renamers_of_operands(2)
+    to_list(1, T.krep[:], ["krepa", "krepb", "krept"], ["gq0"])
+    ts(T.OL[:], T.ramp[:, 0:8:4], T.cf[:, 3:4], 4.0, ALU.add, ALU.mult, ["ramp", "cf3"], ["OL"])
+    renamers(2)
+    after_arrival(0)
+    operands_and_send(1)
+
+    kept_flags()
+    act(T.rbg[:, 0:A], M0.indirect(lb(2)), ACT.Copy, ["M0a", "M0b", "lbu"], quarters("rbb"))
+    act(T.rbg[:, A:2 * A], M0.indirect(la(2)), ACT.Copy, ["M0a", "M0b", "lau"], quarters("rba"))
+    commit(0)
+    mask_by_quarter(T.rbg, T.rbg, 2 * A, [], ["rba", "rbb"])
+    mask_by_quarter(T.odg, T.M0, C, ["M0a", "M0b"], ["od"])
+    mask_by_quarter(T.Pk, T.krep, 2 * A, ["krepa", "krepb"], ["Pk"])
+    to_list(2, T.inv[:], ["inv"], ["gq1"])
+    for i, (l, key) in enumerate(((lb(2), "lbu"), (la(2), "lau"))):
+        tt(T.Pn[:, A * i:A * i + A], T.C0[:].indirect(l), T.mask4[:], ALU.mult, ["C0", key, "mask4"], ["Pn%d" % i])
+    for i in range(2):
+        scan(T.Xn[:, A * i:A * i + A], T.d0n[:, 0:A], T.Pn[:, A * i:A * i + A], 0.0, ALU.mult, ALU.add, ["d0n", "Pn%d" % i], ["Xn%d" % i])
+    slots(T.rbg, 2 * A, RB)
+    cp(T.P[:, 1:4 * A:8], T.Xn[:, 3:2 * A:4], ["Xn0", "Xn1"], ["h0"])
+    cp(T.P[:, 7:4 * A:8], T.Xs[:, 3:2 * A:4], ["Xs"], ["h3"])
+    slots(T.odg, C, quarters("od"))
+    cp(T.m0s[:], T.Xs[:, 3:C:4], ["Xs"], ["m0s"])
+    after_arrival(1)
+    operands_and_send(2)
+
+    kept_flags()
+    mask_by_quarter(T.rbg, T.C0, C, ["C0"], ["rba", "rbb"])
+    commit(1)
+    mask_by_quarter(T.Pk, T.inv, C, ["inv"], ["Pk"])
+    mask_by_quarter(T.odg, T.C1, C, ["C1"], ["od"])
+    slots(T.rbg, C, RB)
+    cp(T.P[:, 5:2 * C:8], T.m0s[:], ["m0s"], ["h2"])
+    ts(T.P[:, 3:2 * C:8], T.Xs[:, 3:C:4], T.d0h[:, 7:8], None, ALU.mult, None, ["Xs", "keep"], ["h1"])
+    tt(T.rbs[:], T.Xs[:, 3:C:4], T.m0s[:], ALU.max, ["Xs", "m0s"], ["rbs"])
+    quant(T.vq[:], T.vp[:], T.vt[:], ["vt"], ["vq"])
+    ts(T.rbs[:], T.rbs[:], 1.0 / 1024, None, ALU.mult, None, ["rbs"], ["rbs"])
+    slots(T.odg, C, quarters("od"))
+    cp(T.P[:, 1:2 * C:8], T.Xs[:, 3:C:4], ["Xs"], ["h0"])
+    after_arrival(2)
+
+    keys = file_keys(R)
+    cut = 32
+
+    def gather_a(i):
+        act(T.Tt[:, 768 * i:768 * i + 16 * cut], window(R).indirect(T.O[:, 48 * i:48 * i + cut]), ACT.Copy, keys + ["O%d" % i], ["Ta%d" % i])
+
+    def gather_v(i):
+        cp(T.Tt[:, 768 * i + 16 * cut:768 * i + 768], window(R).indirect(T.O[:, 48 * i + cut:48 * i + 48]), keys + ["O%d" % i], ["Tb%d" % i])
+
+    def half(i):
+        a, b = 192 * i, 192 * i + 192
+        quant(T.tq[:, a:b], T.tp[:, a:b], T.Tt[:, 4 * a:4 * b], ["Ta%d" % i, "Tb%d" % i], ["tq%d" % i])
+        mm(6 + i, 192, T.vq[:], T.vp[:], T.tq[:, a:b], T.tp[:, a:b], ["vq", "tq%d" % i])
+        dma("S", "outs", T.oc[:, 4 * a:4 * b], T.tq[:, a:b].bitcast(dt.uint8), ["tq%d" % i], [])
+    gather_a(0)
+    for b in range(3):
+        cp(T.Rr[:, 32 * b:32 * b + 32], T.XO[:, 8 * b + 7:2 * C:24], ["XO0", "XO1"], ["Rr%d" % b])
+    op("V", lambda: V.transpose(T.Rt[:], T.Rr[:]), ["Rr0", "Rr1", "Rr2", "Rrt"], ["Rt"])
+    cp(T.omc[:], T.Rt[:].indirect(T.OL[:]), ["Rt", "OL"], ["omc"])
+    for h in range(2):
+        dma("S", "outs", T.om[h:8:2, :], T.omc[:, 16 * h:16 * h + 12], ["omc"], [])
+    gather_v(0)
+    gather_a(1)
+    half(0)
+    gather_v(1)
+    act(T.ys[:, 0:192], T.ps6[:, 0:192], ACT.Copy, [], ["ys0", "ps6"])
+    half(1)
+    cp(T.ys[:, 192:C], T.ps7[:, 0:192], [], ["ys1", "ps7"])
+    for k in range(4):
+        dma("A", "outs", T.osc[4 * k:4 * k + 4, :], T.tp[32 * k:32 * k + 4, :], ["tq0", "tq1"], [])
+    dma("S", "outs", T.y[:], T.ys[:], ["ys0", "ys1"], [])
+
+    count = emit(g, T, ops)
+    g.wait_ge(T.sem.sent, count["sent"])
+    g.wait_ge(T.sem.outs, count["outs"])

@@ -24,9 +24,10 @@ SCRATCH = {
     "d0n": _sb(C, "bfloat16"), "d0h": _sb(2 * C, "bfloat16"),
     "P": _sb(2 * C, HALF), "XO": _sb(2 * C, HALF), "Pn": _sb(2 * A, HALF), "Xn": _sb(2 * A, HALF),
     "M0": _sb(C), "C0": _sb(C), "C1": _sb(C), "m0s": _sb(96), "inv": _sb(C), "krep": _sb(C), "Pk": _sb(C),
-    "rbg": _sb(C), "odg": _sb(C), "Xs": _sb(C), "rbs": _sb(96),
-    "O": _sb(96, "uint16"), "fw": _sb(176), "fk": _sb(A), "wk": _sb(A),
-    "sg": _sb(A), "key": _sb(2), "bc": _sb(32), "tr": _sb(32), "cm": _sb(8), "r8": _sb(8),
+    "rbg": _sb(C), "rbs": _sb(96), "c0s": _sb(96), "kp": _sb(2),
+    "mk": _sb(C, HALF), "mk2": _sb(C, HALF), "mk3": _sb(C, HALF), "Xh": _sb(C, HALF),
+    "O": _sb(96, "uint16"), "fw": _sb(176), "wk": _sb(A),
+    "sg": _sb(A), "key": _sb(2), "bc": _sb(32), "tr": _sb(32), "cm": _sb(8), "r8": _sb(24),
     "Bt": _sb(4 * A, "bfloat16"), "Z": _sb(4 * A, "bfloat16"), "H": _sb(4 * A, "bfloat16"),
     "hq": _sb(A, "float8_e4m3fn_x4"), "hp": _sb(A, "uint8"),
     "Tt": _sb(4 * C, "bfloat16"), "tq": _sb(C, "float8_e4m3fn_x4"), "tp": _sb(C, "uint8"),
@@ -152,7 +153,7 @@ def rank_program(g, core, T, topo):
 
     def afill(out, c, w):
         n = out.shape[1]
-        act(out, T.ramp[:, 0:n], ACT.Identity, ["ramp"], w, scale=0.0, bias=float(c))
+        act(out, T.d0n[:, 0:n], ACT.Identity, ["d0n"], w, scale=0.0, bias=float(c))
 
     def mm(bank, n, lq, lp, rq, rp, r):
         op("T", lambda: PE.matmul_mx(T["ps%d" % bank][:, 0:n], lq, lp, rq, rp, True, True), r, ["ps%d" % bank])
@@ -163,9 +164,9 @@ def rank_program(g, core, T, topo):
         else:
             op("G", lambda: g.iota(out, pattern, base, cm, allow_small_or_imprecise_dtypes=True), [], w)
 
-    def mask_by_quarter(out, in_, n, r, w):
-        for q in range(4):
-            act(out[:, q:n:4], in_[:, q:n:4], ACT.Copy, r + ["mask4"], [k + str(q) for k in w], scale=T.mask4[:, q:q + 1])
+    def mask_by_quarter(out, in_, n, r, w, qs=range(4)):
+        for q in qs:
+            act(out[:, q:n:4], in_[:, q:n:4], ACT.Copy, r + ["mask4"], [w + str(q)], scale=T.mask4[:, q:q + 1])
 
     quarters = lambda k: [k + str(q) for q in range(4)]
     LM, LA, LB, LD = 0, 24, 54, 84
@@ -181,50 +182,37 @@ def rank_program(g, core, T, topo):
     dma("A", "dlb", T.lst[:, LB:LB + 30], T.lb[:], [], ["lb"])
     dma("S", "dla", T.lst[:, LA:LA + 30], T.la[:], [], ["la"])
     dma("S", "dx", T.F[:, 0:4 * C], T.x[:], [], ["x"])
-    dma("S", "dld", T.lst[:, LD:LD + 30], T.ld[:], [], ["ld"])
+    dma("A", "dld", T.lst[:, LD:LD + 30], T.ld[:], [], ["ld"])
     dma("S", "du", T.ut[:], T.u[:], ["m"], ["ut"])
     dma("S", "dws", T.wp[:], T.ws[:], [], ["wp"])
     dma("S", "dwc", T.wq[:].bitcast(dt.uint8), T.wc[:], [], ["wq"])
-    dma("S", "dv", T.vt[:], T.v[:], [], ["vt"])
 
     iota(T.pi[:, 0:1], [[0, 1]], 0, 1, ["pi0"], True)
-    iota(T.em4[:], [[0, 40], [1, 4]], 0, 0, ["em4"])
     iota(T.ramp[:, 0:C], [[1, C]], 0, 0, ["ramp"])
+    iota(T.em4[:], [[0, 40], [1, 4]], 0, 0, ["em4"])
     iota(T.u2i[:], [[2, 4], [0, 2]], 0, 1, ["u2i"], True)
+    fill(T.d0n[:], 1.0, ["d0n"])
     fill(T.d0h[:], 1.0, ["d0h", "keep"])
     iota(T.ramp[:, C:C + R * A], [[1, R * A]], C, 0, ["ramp2"])
     op("G", lambda: g.affine_select(T.eb[:, 0:516], T.d0h[:, 0:516], [[-1, 516]], ALU.is_equal, 0.0, 3, 4), ["d0h", "keep"], ["eb"])
-    fill(T.d0n[:], 1.0, ["d0n"])
     p0 = T.pi[:, 0:1]
+    fill(T.d0n[:, 0:C:4], 0.0, ["d0n"])
+    ts(T.pi[:, 5:6], p0, 4, 6, ALU.logical_shift_right, ALU.bitwise_and, ["pi0"], ["pi5"])
     ts(T.pi[:, 1:2], p0, 3, None, ALU.bitwise_and, None, ["pi0"], ["pi1"])
     ts(T.pi[:, 2:3], p0, 2, 3, ALU.logical_shift_right, ALU.bitwise_and, ["pi0"], ["pi2"])
-    ts(T.pi[:, 5:6], p0, 4, 6, ALU.logical_shift_right, ALU.bitwise_and, ["pi0"], ["pi5"])
+    tt(T.pi[:, 6:7], p0, T.pi[:, 5:6], ALU.add, ["pi0", "pi5"], ["pi6"])
     ts(T.pi[:, 3:4], p0, 15, None, ALU.bitwise_and, None, ["pi0"], ["pi3"])
     ts(T.pi[:, 4:5], p0, 31, None, ALU.bitwise_and, None, ["pi0"], ["pi4"])
-    tt(T.pi[:, 6:7], p0, T.pi[:, 5:6], ALU.add, ["pi0", "pi5"], ["pi6"])
-    fill(T.d0n[:, 0:C:4], 0.0, ["d0n"])
     ts(T.pi[:, 7:8], T.pi[:, 6:7], 7, None, ALU.bitwise_and, None, ["pi6"], ["pi7"])
     fill(T.inv[:], 0.0, ["inv"])
     cp(T.pf[:], T.pi[:], ["pi%d" % i for i in range(8)], ["pf"])
-    ts(T.P[:, 1:2 * C:2], T.d0n[:], 0.0, None, ALU.mult, None, ["d0n"], ["h0", "h1", "h2", "h3"])
-    ts(T.mask4[:], T.em4[:], qcol, None, ALU.is_equal, None, ["em4", "pf"], ["mask4"])
-    act(T.cf[:, 1:2], T.pf[:, 3:4], ACT.Identity, ["pf"], ["cf1"], scale=16.0)
-    ts(T.u2j[:], T.u2i[:], 7, None, ALU.bitwise_and, None, ["u2i"], ["u2j"])
-    ts(T.UL[:, 0:8], T.ramp[:, 0:8], 16.0, None, ALU.mult, None, ["ramp"], ["ULa"])
-    ts(T.UL[:, 8:16], T.u2j[:], 16.0, None, ALU.mult, None, ["u2j"], ["ULb"])
-    ts(T.cf[:, 2:3], T.pf[:, 3:4], 8.0, float(1 - C), ALU.is_ge, ALU.mult, ["pf"], ["cf2"])
-    ts(T.RL[:, 0:24:3], T.ramp[:, 0:16:2], T.cf[:, 1:2], None, ALU.add, None, ["ramp", "cf1"], ["RL0"])
-    ts(T.RL[:, 2:24:3], T.ramp[:, 129:145:2], T.cf[:, 1:2], None, ALU.add, None, ["ramp", "cf1"], ["RL2"])
-    ts(T.RL[:, 1:24:3], T.ramp[:, 256:272:2], T.cf[:, 1:2], T.cf[:, 2:3], ALU.add, ALU.add, ["ramp", "cf1", "cf2"], ["RL1"])
-    act(T.cf[:, 3:4], qcol, ACT.Identity, ["pf"], ["cf3"], scale=8.0, bias=tcol)
-    act(T.cf[:, 4:5], T.pf[:, 7:8], ACT.Identity, ["pf"], ["cf4"], scale=-0.125, bias=A / 2 + 0.875)
     afill(T.b0[:], 1, ["b0", "b0a", "b0b"])
     afill(T.b1[:], 0, ["b1"])
     afill(T.fw[:, 0:1], 0, ["fw0"])
-    afill(T.krep[:, 2 * A:C], 0, ["krept"])
-    afill(T.Rr[:, 96:128], 0, ["Rrt"])
     afill(T.c8[:, 0:7], -100, ["c8a"])
     afill(T.c8[:, 7:8], 0, ["c8b"])
+    afill(T.Rr[:, 96:128], 0, ["Rrt"])
+    act(T.cf[:, 1:2], T.pf[:, 3:4], ACT.Identity, ["pf"], ["cf1"], scale=16.0)
 
     def offsets(src, lo, n, r, w):
         ts(T.O[:, lo:lo + n], src, 4.0, tcol, ALU.mult, ALU.add, r + ["pf"], [w])
@@ -258,22 +246,23 @@ def rank_program(g, core, T, topo):
         act(T.krep[:, 0:A], T.inv[:].indirect(lb(t)), ACT.Copy, ["inv", "lbu"], ["krepb"])
         act(T.krep[:, A:2 * A], T.inv[:].indirect(la(t)), ACT.Copy, ["inv", "lau"], ["krepa"])
 
-    def to_list(t, src, r, after):
+    def to_list(t, src, r):
         act(T["ro%d" % t][:], src.indirect(T.RL[:]), ACT.Copy, r + ["RL0", "RL1", "RL2"], ["ro%d" % t])
-        dma("S", "dk%d" % t, T["kl%d" % t][:], T["ro%d" % t][0:128:16, :], ["ro%d" % t] + after, ["kl%d" % t])
+        dma("S", "dk%d" % t, T["kl%d" % t][:], T["ro%d" % t][0:128:16, :], ["ro%d" % t], ["kl%d" % t])
 
-    def slots(src, n, r):
-        scan(T.Xs[:, 0:n], T.d0n[:, 0:n], src[:, 0:n], 0.0, ALU.mult, ALU.add, r + ["d0n"], ["Xs"])
+    def slots(out, src, n, r, w):
+        scan(out, T.d0n[:, 0:n], src[:, 0:n], 0.0, ALU.mult, ALU.add, r + ["d0n"], w)
+
+    kp = lambda t: T.kp[:, t:t + 1]
+    keep = lambda t: T.r8[:, 8 * t + 7:8 * t + 8]
 
     def commit(t):
         lo = C + A * t
-        tt(T.wk[:], T.fk[:], T.ramp[:, lo:lo + A], ALU.min, ["fk", "ramp2"], ["wk"])
+        tt(T.wk[:], T.fw[:, 1:A + 1], T.ramp[:, lo:lo + A], ALU.min, ["fw", "ramp2"], ["wk"])
+        ts(kp(t), keep(t), 1.0, None, ALU.min, None, ["r8%d" % t], ["kp%d" % t])
         cp(T["C%d" % t][:].indirect(ld(t)), T.wk[:], ["wk", "ldu"], ["C%d" % t])
 
-    def kept_flags():
-        act(T.fk[:], T.fw[:, 1:A + 1], ACT.Copy, ["fw", "r8"], ["fk"], scale=T.r8[:, 7:8])
-
-    def after_arrival(t):
+    def after_arrival(t, a1=None, a2=None, v1=None):
         gq, gp, n = T["gq%d" % t][:], T["gp%d" % t][:], (C if t == R - 1 else 2 * A)
         h = n // 2
         for b in range(4):
@@ -284,7 +273,11 @@ def rank_program(g, core, T, topo):
                 ts(T.H[:, b:4 * A:4], bank, 0.0, 0.015625, ALU.max, ALU.mult, [], ["H%d" % b, "ps%d" % b])
             else:
                 act(T.H[:, b:4 * A:4], bank, ACT.Relu, [], ["H%d" % b, "ps%d" % b], scale=0.015625)
+        if a1:
+            a1()
         quant(T.hq[:], T.hp[:], T.H[:], quarters("H"), ["hq"])
+        if v1:
+            v1()
         mm(5, A, T.u2q[:, 128:256], T.u2p[:, 128:256], T.hq[:], T.hp[:], ["u2q", "u2p", "hq"])
         mm(4, A, T.u2q[:, 0:128], T.u2p[:, 0:128], T.hq[:], T.hp[:], ["u2q", "u2p", "hq"])
         for b in range(4):
@@ -295,6 +288,8 @@ def rank_program(g, core, T, topo):
         lo = 4 * (C + A * t)
         for b in range(4):
             act(T.F[:, lo + b:lo + 4 * A:4], T["ps%d" % b][:, 0:A], ACT.Copy, [], ["F%d%d" % (t, b), "ps%d" % b])
+        if a2:
+            a2()
         ts(T.fw[:, 1:A + 1], T.ps4[:, 0:A], 0.0, 1024.0, ALU.is_ge, ALU.mult, [], ["fw", "ps4"])
         cuts = [0, 4 if n < C else 6, n // 32, n // 32 + 6, n // 16]
 
@@ -308,124 +303,152 @@ def rank_program(g, core, T, topo):
         flags(1)
         ts(T.cm[:], T.tr[:, 0:8], T.tr[:, 8:9], T.tr[:, 9:10], ALU.subtract, ALU.is_gt, ["tr"], ["cm"])
         flags(2)
-        scan(T.r8[:], T.cm[:], T.c8[:], -1.0, ALU.add, ALU.max, ["cm", "c8a", "c8b"], ["r8"])
+        scan(T.r8[:, 8 * t:8 * t + 8], T.cm[:], T.c8[:], -1.0, ALU.add, ALU.max, ["cm", "c8a", "c8b"], ["r8%d" % t])
         flags(3)
-        ts(T.d0h[:, 7:2 * n:8], T.d0n[:, 1:n:4], T.r8[:, 7:8], None, ALU.min, None, ["d0n", "r8"], ["keep"])
+        ts(T.d0h[:, 7:2 * n:8], T.d0n[:, 1:n:4], keep(t), None, ALU.min, None, ["d0n", "r8%d" % t], ["keep"])
         if t == R - 1:
-            ts(T.P[:, 7:2 * n:8], T.rbs[:], T.r8[:, 7:8], 1024.0, ALU.subtract, ALU.mult, ["rbs", "r8"], ["h3"])
+            ts(T.P[:, 7:2 * n:8], T.rbs[:], keep(t), 1024.0, ALU.subtract, ALU.mult, ["rbs", "r8%d" % t], ["h3"])
         for i in range(2):
             a, b = 2 * h * i, 2 * h * (i + 1)
             scan(T.XO[:, a:b], T.d0h[:, a:b], T.P[:, a:b], 0.0, ALU.mult, ALU.max,
                  ["d0h", "keep", "h0", "h1", "h2", "h3", "f%d" % (2 * i), "f%d" % (2 * i + 1)], ["XO%d" % i])
             offsets(T.XO[:, a + 7:b:8], i * h // 4, h // 4, ["XO%d" % i], "O%d" % i)
 
+    HS = ["h0", "h1", "h2", "h3"]
+    MK = ["M0a", "M0b"]
     cp(T.lu[:, LM:LM + 24], T.lst[:, LM:LM + 24], ["m"], ["mu"])
-    cp(T.M0[:, 0:192], T.ramp[:, 0:C].indirect(T.lu[:, 0:12]), ["ramp", "mu"], ["M0a"])
-    act(T.M0[:, 192:C], T.ramp[:, 0:C].indirect(T.lu[:, 12:24]), ACT.Copy, ["ramp", "mu"], ["M0b"])
-    for i, (lo, l, key) in enumerate(((LB, lb(0), "lb"), (LA, la(0), "la"))):
-        cp(T.lu[:, lo:lo + 30], T.lst[:, lo:lo + 30], [key], [key + "u"])
-        tt(T.Pn[:, A * i:A * i + A], M0.indirect(l), T.mask4[:], ALU.mult, ["M0a", "M0b", key + "u", "mask4"], ["Pn%d" % i])
-        scan(T.Xn[:, A * i:A * i + A], T.d0n[:, 0:A], T.Pn[:, A * i:A * i + A], 0.0, ALU.mult, ALU.add, ["d0n", "Pn%d" % i], ["Xn%d" % i])
-        offsets(T.Xn[:, A * i + 3:A * i + A:4], 40 * i, 40, ["Xn%d" % i], "O%d" % i)
-    act(T.rbg[:, 0:A], M0.indirect(lb(1)), ACT.Copy, ["M0a", "M0b", "lbu"], quarters("rbb"))
+    ts(T.mask4[:], T.em4[:], qcol, None, ALU.is_equal, None, ["em4", "pf"], ["mask4"])
+    act(T.M0[:, A:C], T.ramp[:, 0:C].indirect(T.lu[:, 10:24]), ACT.Copy, ["ramp", "mu"], ["M0b"])
+    cp(T.M0[:, 0:A], T.ramp[:, 0:C].indirect(T.lu[:, 0:10]), ["ramp", "mu"], ["M0a"])
+    cp(T.lu[:, LA:LD], T.lst[:, LA:LD], ["la", "lb"], ["lau", "lbu"])
+    tt(T.Pn[:, 0:A], M0.indirect(lb(0)), T.mask4[:], ALU.mult, MK + ["lbu", "mask4"], ["Pn0"])
+    ts(T.cf[:, 2:3], T.pf[:, 3:4], 8.0, float(1 - C), ALU.is_ge, ALU.mult, ["pf"], ["cf2"])
+    slots(T.Xn[:, 0:A], T.Pn, A, ["Pn0"], ["Xn0"])
+    cp(T.lu[:, LD:LD + 30], T.lst[:, LD:LD + 30], ["ld"], ["ldu"])
+    offsets(T.Xn[:, 3:A:4], 0, 40, ["Xn0"], "O0")
+    tt(T.Pn[:, A:2 * A], M0.indirect(la(0)), T.mask4[:], ALU.mult, MK + ["lau", "mask4"], ["Pn1"])
+    ts(T.u2j[:], T.u2i[:], 7, None, ALU.bitwise_and, None, ["u2i"], ["u2j"])
+    scan(T.Xn[:, A:2 * A], T.d0n[:, 0:A], T.Pn[:, A:2 * A], 0.0, ALU.mult, ALU.add, ["d0n", "Pn1"], ["Xn1"])
+    ts(T.UL[:, 0:8], T.ramp[:, 0:8], 16.0, None, ALU.mult, None, ["ramp"], ["ULa"])
+    offsets(T.Xn[:, A + 3:2 * A:4], 40, 40, ["Xn1"], "O1")
+    renamers(0)
+
+    def first_places(l, key, lo):
+        act(T.rbg[:, lo:lo + A], M0.indirect(l), ACT.Copy, MK + [key], ["rb%d" % lo])
+    first_places(lb(1), "lbu", 0)
+    first_places(la(1), "lau", A)
     operands_and_send(0)
 
-    RB = quarters("rba") + quarters("rbb")
+    RB = ["rb0", "rb%d" % A]
     iota(T.C0[:], [[0, C]], 0, 0, ["C0"])
     iota(T.C1[:], [[0, C]], 0, 0, ["C1"])
-    cp(T.lu[:, LD:LD + 30], T.lst[:, LD:LD + 30], ["ld"], ["ldu"])
-    renamers(0)
-    act(T.rbg[:, A:2 * A], M0.indirect(la(1)), ACT.Copy, ["M0a", "M0b", "lau"], quarters("rba"))
-    mask_by_quarter(T.rbg, T.rbg, 2 * A, [], ["rba", "rbb"])
     renamers_of_operands(1)
-    to_list(0, T.krep[:], ["krepa", "krepb", "krept"], [])
+    afill(T.krep[:, 2 * A:C], 0, ["krept"])
+    ts(T.RL[:, 0:24:3], T.ramp[:, 0:16:2], T.cf[:, 1:2], None, ALU.add, None, ["ramp", "cf1"], ["RL0"])
+    ts(T.RL[:, 2:24:3], T.ramp[:, 129:145:2], T.cf[:, 1:2], None, ALU.add, None, ["ramp", "cf1"], ["RL2"])
+    ts(T.RL[:, 1:24:3], T.ramp[:, 256:272:2], T.cf[:, 1:2], T.cf[:, 2:3], ALU.add, ALU.add, ["ramp", "cf1", "cf2"], ["RL1"])
+    ts(T.UL[:, 8:16], T.u2j[:], 16.0, None, ALU.mult, None, ["u2j"], ["ULb"])
+    to_list(0, T.krep[:], ["krepa", "krepb", "krept"])
+    dma("S", "dv", T.vt[:], T.v[:], ["gq0"], ["vt"])
     quant(T.uq[:], T.up[:], T.ut[:], ["ut"], ["uq"])
     fill(T.d0h[:, 0:2 * C:8], 0.0, ["d0h"])
     cp(T.u2q[:].bitcast(dt.uint32), T.uq[:].bitcast(dt.uint32).indirect(T.UL[:]), ["uq", "ULa", "ULb"], ["u2q"])
+    mask_by_quarter(T.mk, T.rbg, 2 * A, RB, "mk")
+    act(T.cf[:, 4:5], T.pf[:, 7:8], ACT.Identity, ["pf"], ["cf4"], scale=-0.125, bias=A / 2 + 0.875)
     act(T.u2p[:], T.up[:].indirect(T.UL[:]), ACT.Copy, ["uq", "ULa", "ULb"], ["u2p"])
-    mask_by_quarter(T.Pk, T.krep, 2 * A, ["krepa", "krepb"], ["Pk"])
-    slots(T.rbg, 2 * A, RB)
+    act(T.cf[:, 3:4], qcol, ACT.Identity, ["pf"], ["cf3"], scale=8.0, bias=tcol)
     ts(T.cf[:, 5:6], T.pf[:, 4:5], 9.0, 4095.0, ALU.is_equal, ALU.mult, ["pf"], ["cf5"])
-    cp(T.P[:, 7:4 * A:8], T.Xs[:, 3:2 * A:4], ["Xs"], ["h3"])
+    tt(T.Pk[:, 0:A], T.krep[:, 0:A], T.mask4[:], ALU.mult, ["krepb", "mask4"], ["Pk0", "Pk1"])
     ts(T.b0[:, 16:17], T.pf[:, 4:5], 8.0, T.cf[:, 5:6], ALU.not_equal, ALU.add, ["pf", "cf5"], ["b0b"])
     ts(T.b0[:, 0:1], T.cf[:, 5:6], -4096.0, 1.0 / 8192, ALU.add, ALU.mult, ["cf5"], ["b0a"])
-    renamers(1)
-    ts(T.b1[:, 0:1], T.cf[:, 4:5], T.b0[:, 0:1], -2.0, ALU.mult, ALU.mult, ["cf4", "b0a"], ["b1"])
+    tt(T.Pk[:, A:2 * A], T.krep[:, A:2 * A], T.mask4[:], ALU.mult, ["krepa", "mask4"], ["Pk2", "Pk3"])
     for b in range(4):
         quant(T.eq[:, 128 * b:128 * b + 128], T.ep[:, 128 * b:128 * b + 128], T.eb[:, 3 - b:515 - b], ["eb"], ["eq%d" % b])
-    renamers_of_operands(2)
-    to_list(1, T.krep[:], ["krepa", "krepb", "krept"], ["gq0"])
-    ts(T.OL[:], T.ramp[:, 0:8:4], T.cf[:, 3:4], 4.0, ALU.add, ALU.mult, ["ramp", "cf3"], ["OL"])
-    renamers(2)
-    after_arrival(0)
+    slots(T.P[:, 1:4 * A:2], T.mk, 2 * A, quarters("mk"), HS)
+    ts(T.b1[:, 0:1], T.cf[:, 4:5], T.b0[:, 0:1], -2.0, ALU.mult, ALU.mult, ["cf4", "b0a"], ["b1"])
+    after_arrival(0, lambda: first_places(lb(2), "lbu", 0), lambda: first_places(la(2), "lau", A))
     operands_and_send(1)
 
-    kept_flags()
-    act(T.rbg[:, 0:A], M0.indirect(lb(2)), ACT.Copy, ["M0a", "M0b", "lbu"], quarters("rbb"))
-    act(T.rbg[:, A:2 * A], M0.indirect(la(2)), ACT.Copy, ["M0a", "M0b", "lau"], quarters("rba"))
+    mask_by_quarter(T.mk, T.rbg, 2 * A, RB, "mk")
+    renamers(1)
+    renamers_of_operands(2)
+    to_list(1, T.krep[:], ["krepa", "krepb", "krept"])
     commit(0)
-    mask_by_quarter(T.rbg, T.rbg, 2 * A, [], ["rba", "rbb"])
-    mask_by_quarter(T.odg, T.M0, C, ["M0a", "M0b"], ["od"])
-    mask_by_quarter(T.Pk, T.krep, 2 * A, ["krepa", "krepb"], ["Pk"])
-    to_list(2, T.inv[:], ["inv"], ["gq1"])
+    mask_by_quarter(T.Pk, T.krep, 2 * A, ["krepa", "krepb"], "Pk")
+    slots(T.P[:, 1:4 * A:2], T.mk, 2 * A, quarters("mk"), HS)
     for i, (l, key) in enumerate(((lb(2), "lbu"), (la(2), "lau"))):
         tt(T.Pn[:, A * i:A * i + A], T.C0[:].indirect(l), T.mask4[:], ALU.mult, ["C0", key, "mask4"], ["Pn%d" % i])
-    for i in range(2):
-        scan(T.Xn[:, A * i:A * i + A], T.d0n[:, 0:A], T.Pn[:, A * i:A * i + A], 0.0, ALU.mult, ALU.add, ["d0n", "Pn%d" % i], ["Xn%d" % i])
-    slots(T.rbg, 2 * A, RB)
-    cp(T.P[:, 1:4 * A:8], T.Xn[:, 3:2 * A:4], ["Xn0", "Xn1"], ["h0"])
-    cp(T.P[:, 7:4 * A:8], T.Xs[:, 3:2 * A:4], ["Xs"], ["h3"])
-    slots(T.odg, C, quarters("od"))
-    cp(T.m0s[:], T.Xs[:, 3:C:4], ["Xs"], ["m0s"])
-    after_arrival(1)
+
+    def round0_places():
+        slots(T.Xn[:], T.Pn, 2 * A, ["Pn0", "Pn1"], ["Xn0", "Xn1"])
+        ts(T.OL[:], T.ramp[:, 0:8:4], T.cf[:, 3:4], 4.0, ALU.add, ALU.mult, ["ramp", "cf3"], ["OL"])
+        ts(T.P[:, 1:4 * A:8], T.Xn[:, 3:2 * A:4], kp(0), None, ALU.mult, None, ["Xn0", "Xn1", "kp0"], ["h0"])
+    after_arrival(1, lambda: mask_by_quarter(T.mk, T.M0, C, MK, "mk", (0, 1)),
+                  lambda: mask_by_quarter(T.mk, T.M0, C, MK, "mk", (2, 3)), round0_places)
     operands_and_send(2)
 
-    kept_flags()
-    mask_by_quarter(T.rbg, T.C0, C, ["C0"], ["rba", "rbb"])
+    mask_by_quarter(T.mk2, T.C0, C, ["C0"], "mkb")
+    renamers(2)
+    to_list(2, T.inv[:], ["inv"])
     commit(1)
-    mask_by_quarter(T.Pk, T.inv, C, ["inv"], ["Pk"])
-    mask_by_quarter(T.odg, T.C1, C, ["C1"], ["od"])
-    slots(T.rbg, C, RB)
-    cp(T.P[:, 5:2 * C:8], T.m0s[:], ["m0s"], ["h2"])
-    ts(T.P[:, 3:2 * C:8], T.Xs[:, 3:C:4], T.d0h[:, 7:8], None, ALU.mult, None, ["Xs", "keep"], ["h1"])
-    tt(T.rbs[:], T.Xs[:, 3:C:4], T.m0s[:], ALU.max, ["Xs", "m0s"], ["rbs"])
-    quant(T.vq[:], T.vp[:], T.vt[:], ["vt"], ["vq"])
+    mask_by_quarter(T.Pk, T.inv, C, ["inv"], "Pk", (0, 1))
+    mask_by_quarter(T.mk3, T.C1, C, ["C1"], "mkc")
+    slots(T.Xh[:], T.mk, C, quarters("mk"), ["Xh"])
+    slots(T.XO[:, 0:C], T.mk2, C, quarters("mkb"), ["XO0", "XO1"])
+    cp(T.m0s[:], T.Xh[:, 3:C:4], ["Xh"], ["m0s"])
+    ts(T.c0s[:], T.XO[:, 3:C:4], kp(0), None, ALU.mult, None, ["XO0", "XO1", "kp0"], ["c0s"])
+    cp(T.P[:, 5:2 * C:8], T.Xh[:, 3:C:4], ["Xh"], ["h2"])
+    tt(T.rbs[:], T.c0s[:], T.m0s[:], ALU.max, ["c0s", "m0s"], ["rbs"])
+    ts(T.P[:, 3:2 * C:8], T.XO[:, 3:C:4], kp(0), kp(1), ALU.mult, ALU.mult, ["XO0", "XO1", "kp0", "kp1"], ["h1"])
     ts(T.rbs[:], T.rbs[:], 1.0 / 1024, None, ALU.mult, None, ["rbs"], ["rbs"])
-    slots(T.odg, C, quarters("od"))
-    cp(T.P[:, 1:2 * C:8], T.Xs[:, 3:C:4], ["Xs"], ["h0"])
-    after_arrival(2)
+
+    def round1_places():
+        slots(T.Xh[:], T.mk3, C, quarters("mkc"), ["Xh"])
+        ts(T.P[:, 1:2 * C:8], T.Xh[:, 3:C:4], kp(1), None, ALU.mult, None, ["Xh", "kp1"], ["h0"])
+    after_arrival(2, lambda: mask_by_quarter(T.Pk, T.inv, C, ["inv"], "Pk", (2, 3)), None, round1_places)
 
     keys = file_keys(R)
-    cut = 32
 
-    def gather_a(i):
-        act(T.Tt[:, 768 * i:768 * i + 16 * cut], window(R).indirect(T.O[:, 48 * i:48 * i + cut]), ACT.Copy, keys + ["O%d" % i], ["Ta%d" % i])
+    def gather_a(a, b, r, w):
+        act(T.Tt[:, 16 * a:16 * b], window(R).indirect(T.O[:, a:b]), ACT.Copy, keys + r, [w])
 
-    def gather_v(i):
-        cp(T.Tt[:, 768 * i + 16 * cut:768 * i + 768], window(R).indirect(T.O[:, 48 * i + cut:48 * i + 48]), keys + ["O%d" % i], ["Tb%d" % i])
+    def gather_v(a, b, r, w):
+        cp(T.Tt[:, 16 * a:16 * b], window(R).indirect(T.O[:, a:b]), keys + r, [w])
 
-    def half(i):
-        a, b = 192 * i, 192 * i + 192
-        quant(T.tq[:, a:b], T.tp[:, a:b], T.Tt[:, 4 * a:4 * b], ["Ta%d" % i, "Tb%d" % i], ["tq%d" % i])
-        mm(6 + i, 192, T.vq[:], T.vp[:], T.tq[:, a:b], T.tp[:, a:b], ["vq", "tq%d" % i])
+    def piece(i, r):
+        a, b = 128 * i, 128 * i + 128
+        quant(T.tq[:, a:b], T.tp[:, a:b], T.Tt[:, 4 * a:4 * b], r, ["tq%d" % i])
+        mm(5 + i, 128, T.vq[:], T.vp[:], T.tq[:, a:b], T.tp[:, a:b], ["vq", "tq%d" % i])
         dma("S", "outs", T.oc[:, 4 * a:4 * b], T.tq[:, a:b].bitcast(dt.uint8), ["tq%d" % i], [])
-    gather_a(0)
+
+    def y_out(q, i):
+        a, b = 128 * i, 128 * i + 128
+        bank = "ps%d" % (5 + i)
+        if q == "A":
+            act(T.ys[:, a:b], T[bank][:, 0:128], ACT.Copy, [], ["ys%d" % i, bank])
+        else:
+            cp(T.ys[:, a:b], T[bank][:, 0:128], [], ["ys%d" % i, bank])
+        dma(q, "outs", T.y[:, a:b], T.ys[:, a:b], ["ys%d" % i], [])
+    gather_a(0, 20, ["O0"], "Ta")
+    gather_v(20, 32, ["O0"], "Tb")
+    gather_a(32, 64, ["O0", "O1"], "Tc")
+    quant(T.vq[:], T.vp[:], T.vt[:], ["vt"], ["vq"])
+    piece(0, ["Ta", "Tb"])
+    gather_v(64, 80, ["O1"], "Td")
+    gather_a(80, 96, ["O1"], "Te")
+    y_out("S", 0)
+    piece(1, ["Tc"])
     for b in range(3):
         cp(T.Rr[:, 32 * b:32 * b + 32], T.XO[:, 8 * b + 7:2 * C:24], ["XO0", "XO1"], ["Rr%d" % b])
+    piece(2, ["Td", "Te"])
+    y_out("A", 1)
     op("V", lambda: V.transpose(T.Rt[:], T.Rr[:]), ["Rr0", "Rr1", "Rr2", "Rrt"], ["Rt"])
+    y_out("S", 2)
     cp(T.omc[:], T.Rt[:].indirect(T.OL[:]), ["Rt", "OL"], ["omc"])
+    for k in range(4):
+        dma("A", "outs", T.osc[4 * k:4 * k + 4, :], T.tp[32 * k:32 * k + 4, :], ["tq0", "tq1", "tq2"], [])
     for h in range(2):
         dma("S", "outs", T.om[h:8:2, :], T.omc[:, 16 * h:16 * h + 12], ["omc"], [])
-    gather_v(0)
-    gather_a(1)
-    half(0)
-    gather_v(1)
-    act(T.ys[:, 0:192], T.ps6[:, 0:192], ACT.Copy, [], ["ys0", "ps6"])
-    half(1)
-    cp(T.ys[:, 192:C], T.ps7[:, 0:192], [], ["ys1", "ps7"])
-    for k in range(4):
-        dma("A", "outs", T.osc[4 * k:4 * k + 4, :], T.tp[32 * k:32 * k + 4, :], ["tq0", "tq1"], [])
-    dma("S", "outs", T.y[:], T.ys[:], ["ys0", "ys1"], [])
 
     count = emit(g, T, ops)
     g.wait_ge(T.sem.sent, count["sent"])

@@ -14,38 +14,42 @@ SCRATCH = {
     "F": _sb(4 * (C + R * A), "bfloat16"), "ut": _sb(512, "bfloat16"), "vt": _sb(512, "bfloat16"),
     "wq": _sb(512, "float8_e4m3fn_x4"), "wp": _sb(512, "uint8"),
     "uq": _sb(128, "float8_e4m3fn_x4"), "up": _sb(128, "uint8"),
-    "u2q": _sb(256, "float8_e4m3fn_x4"), "u2p": _sb(256, "uint8"),
+    "u2q": _sb(128, "float8_e4m3fn_x4"), "u2p": _sb(128, "uint8"),
     "vq": _sb(128, "float8_e4m3fn_x4"), "vp": _sb(128, "uint8"),
     "eb": _sb(520, "bfloat16"), "eq": _sb(512, "float8_e4m3fn_x4"), "ep": _sb(512, "uint8"),
-    "ramp": _sb(C + R * A), "pi": _sb(8, "int32"), "pf": _sb(8), "cf": _sb(8),
-    "em4": _sb(A), "mask4": _sb(A), "u2i": _sb(8, "int32"), "u2j": _sb(8, "int32"),
-    "RL": _sb(24, "uint16"), "UL": _sb(16, "uint16"), "OL": _sb(2, "uint16"),
-    "b0": _sb(32), "b1": _sb(32), "c8": _sb(8),
-    "d0n": _sb(C, "bfloat16"), "d0h": _sb(2 * C, "bfloat16"),
-    "P": _sb(2 * C, HALF), "XO": _sb(2 * C, HALF), "Pn": _sb(2 * A, HALF), "Xn": _sb(2 * A, HALF),
-    "M0": _sb(C), "C0": _sb(C), "C1": _sb(C), "m0s": _sb(96), "inv": _sb(C), "krep": _sb(C), "Pk": _sb(C),
-    "rbg": _sb(C), "rbs": _sb(96), "c0s": _sb(96), "kp": _sb(2),
-    "mk": _sb(C, HALF), "mk2": _sb(C, HALF), "mk3": _sb(C, HALF), "Xh": _sb(C, HALF),
-    "O": _sb(96, "uint16"), "fw": _sb(176), "wk": _sb(A),
-    "sg": _sb(A), "key": _sb(2), "bc": _sb(32), "tr": _sb(32), "cm": _sb(8), "r8": _sb(24),
+    "ones": _sb(520, "bfloat16"), "pp": _sb(A), "true": _sb(C + R * A),
+    "pi": _sb(8, "int32"), "pf": _sb(8), "cf": _sb(8),
+    "mask4": _sb(A, "bfloat16"), "u2i": _sb(8, "int32"), "u2j": _sb(8, "int32"), "UL": _sb(8, "uint16"), "XL": _sb(4, "uint16"),
+    "b0": _sb(32), "k8": _sb(16), "key": _sb(2), "bc": _sb(32), "tr": _sb(32), "sg": _sb(R * 176, "bfloat16"),
+    "em": _sb(A, "bfloat16"), "Pn": _sb(2 * A, HALF), "Xn": _sb(2 * A, HALF), "O0": _sb(80, "uint16"),
+    "M0": _sb(C), "inv": _sb(3 * C, "bfloat16"),
+    "ln": _sb(96, "int32"), "ra": _sb(96), "rb": _sb(96),
+    "k0": _sb(72, "uint16"), "k1": _sb(96, "uint16"), "k2": _sb(16, "uint16"),
+    "ro1": _sb(6 * A), "ro2": _sb(4 * A), "ro3": _sb(2 * A),
+    "own1": _sb(60), "crs1": _sb(60), "own2": _sb(40), "crs2": _sb(40), "own3": _sb(20), "crs3": _sb(20),
+    "ownA": _sb(72, "bfloat16"), "crsA": _sb(72, "bfloat16"),
+    "Rc": _sb(C, "bfloat16"), "Tc": _sb(C, "bfloat16"), "Rp": _sb(C, "bfloat16"), "Tp": _sb(C, "bfloat16"),
+    "Rq": _sb(C, "bfloat16"), "Tq": _sb(C, "bfloat16"),
+    "DD": _sb(680), "Dp": _sb(72), "Dq": _sb(72), "D11": _sb(72), "D21": _sb(72),
+    "Xc": _sb(72), "Xp": _sb(72), "Xq": _sb(72), "w1": _sb(24), "w2": _sb(24), "O": _sb(5 * 24, "uint16"),
     "Bt": _sb(4 * A, "bfloat16"), "Z": _sb(4 * A, "bfloat16"), "H": _sb(4 * A, "bfloat16"),
     "hq": _sb(A, "float8_e4m3fn_x4"), "hp": _sb(A, "uint8"),
     "Tt": _sb(4 * C, "bfloat16"), "tq": _sb(C, "float8_e4m3fn_x4"), "tp": _sb(C, "uint8"),
-    "ys": _sb(C), "Rr": _sb(128), "Rt": _sb(128), "omc": _sb(32),
+    "ys": _sb(C), "omr": _sb(C),
 }
 for _t in range(R):
     SCRATCH["zq%d" % _t] = _sb(A, "float8_e4m3fn_x4")
     SCRATCH["zp%d" % _t] = _sb(A, "uint8")
     SCRATCH["gq%d" % _t] = _sb(A, "float8_e4m3fn_x4")
     SCRATCH["gp%d" % _t] = _sb(A, "uint8")
-    SCRATCH["ro%d" % _t] = _sb(C)
-    SCRATCH["kl%d" % _t] = _sb(24)
-    SCRATCH["KO%d" % _t] = _sb(24, "uint16")
+    SCRATCH["KX%d" % _t] = _sb(24, "uint16")
+    SCRATCH["KP%d" % _t] = _sb(24, "uint16")
 for _b in range(8):
     SCRATCH["ps%d" % _b] = ("psum", [128, 512], "float32")
 
-SEMAPHORES = ["cV", "cA", "cT", "cG", "sent", "outs", "arr0", "arr1", "arr2",
-              "dm", "dla", "dlb", "dld", "dx", "du", "dv", "dwc", "dws", "dk0", "dk1", "dk2"]
+SEMAPHORES = (["cV", "cA", "cT", "cG", "sent", "outs", "arr0", "arr1", "arr2",
+               "dm", "dla", "dlb", "dld", "dx", "du", "dv", "dwc", "dws"]
+              + ["d%s%s%d" % (k, n, h) for k in "oc" for n in "123A" for h in range(2)])
 
 ALU = AluOpType
 ACT = ActivationFunctionType
@@ -148,12 +152,20 @@ def rank_program(g, core, T, topo):
     def quant(q, s, t, r, w):
         op("V", lambda: V.quantize_mx(q, s, t), r, w)
 
+    def turn(out, in_, r, w):
+        op("V", lambda: V.transpose(out, in_), r, w)
+
     def act(out, in_, func, r, w, **kw):
         op("A", lambda: S.activation(out, in_, func, **kw), r, w)
 
+    def acp(out, in_, r, w):
+        act(out, in_, ACT.Copy, r, w)
+
+    def aff(out, in_, scale, bias, r, w):
+        act(out, in_, ACT.Identity, r, w, scale=scale, bias=bias)
+
     def afill(out, c, w):
-        n = out.shape[1]
-        act(out, T.d0n[:, 0:n], ACT.Identity, ["d0n"], w, scale=0.0, bias=float(c))
+        aff(out, T.ones[:, 0:out.shape[1]], 0.0, float(c), ["ones"], w)
 
     def mm(bank, n, lq, lp, rq, rp, r):
         op("T", lambda: PE.matmul_mx(T["ps%d" % bank][:, 0:n], lq, lp, rq, rp, True, True), r, ["ps%d" % bank])
@@ -164,19 +176,15 @@ def rank_program(g, core, T, topo):
         else:
             op("G", lambda: g.iota(out, pattern, base, cm, allow_small_or_imprecise_dtypes=True), [], w)
 
-    def mask_by_quarter(out, in_, n, r, w, qs=range(4)):
-        for q in qs:
-            act(out[:, q:n:4], in_[:, q:n:4], ACT.Copy, r + ["mask4"], [w + str(q)], scale=T.mask4[:, q:q + 1])
-
     quarters = lambda k: [k + str(q) for q in range(4)]
-    LM, LA, LB, LD = 0, 24, 54, 84
+    LM, LB, LA, LD = 0, 24, 54, 84
     la = lambda t: T.lu[:, LA + 10 * t:LA + 10 * t + 10]
     lb = lambda t: T.lu[:, LB + 10 * t:LB + 10 * t + 10]
-    ld = lambda t: T.lu[:, LD + 10 * t:LD + 10 * t + 10]
-    M0 = T.M0[:]
-    tcol, qcol = T.pf[:, 1:2], T.pf[:, 2:3]
+    M0, p0, ramp = T.M0[:], T.pi[:, 0:1], T.true[:, 0:C]
+    tcol, qcol, run, half, lane, row = (T.pf[:, i:i + 1] for i in (1, 2, 3, 4, 5, 6))
     file_keys = lambda t: ["x"] + ["F%d%d" % (s, b) for s in range(t) for b in range(4)]
     window = lambda t: T.F[:, 0:4 * (C + A * t)]
+    base = lambda t: float(C + A * t - 1)
 
     dma("S", "dm", T.lst[:, LM:LM + 24], T.m[:], [], ["m"])
     dma("A", "dlb", T.lst[:, LB:LB + 30], T.lb[:], [], ["lb"])
@@ -187,48 +195,26 @@ def rank_program(g, core, T, topo):
     dma("S", "dws", T.wp[:], T.ws[:], [], ["wp"])
     dma("S", "dwc", T.wq[:].bitcast(dt.uint8), T.wc[:], [], ["wq"])
 
-    iota(T.pi[:, 0:1], [[0, 1]], 0, 1, ["pi0"], True)
-    iota(T.ramp[:, 0:C], [[1, C]], 0, 0, ["ramp"])
-    iota(T.em4[:], [[0, 40], [1, 4]], 0, 0, ["em4"])
+    iota(p0, [[0, 1]], 0, 1, ["pi0"], True)
+    fill(T.ones[:], 1.0, ["ones"])
+    iota(T.em[:], [[0, 40], [512, 4]], 0, 0, ["em"])
+    op("G", lambda: g.affine_select(T.eb[:, 0:516], T.ones[:, 0:516], [[-1, 516]], ALU.is_equal, 0.0, 3, 4), ["ones"], ["eb"])
     iota(T.u2i[:], [[2, 4], [0, 2]], 0, 1, ["u2i"], True)
-    fill(T.d0n[:], 1.0, ["d0n"])
-    fill(T.d0h[:], 1.0, ["d0h", "keep"])
-    iota(T.ramp[:, C:C + R * A], [[1, R * A]], C, 0, ["ramp2"])
-    op("G", lambda: g.affine_select(T.eb[:, 0:516], T.d0h[:, 0:516], [[-1, 516]], ALU.is_equal, 0.0, 3, 4), ["d0h", "keep"], ["eb"])
-    p0 = T.pi[:, 0:1]
-    fill(T.d0n[:, 0:C:4], 0.0, ["d0n"])
-    ts(T.pi[:, 5:6], p0, 4, 6, ALU.logical_shift_right, ALU.bitwise_and, ["pi0"], ["pi5"])
+    iota(T.pp[:], [[1, 16], [16, 10]], 1, 0, ["pp"])
+    iota(T.DD[:], [[0, 680]], 0, 0, ["DD"])
+    scan(ramp, T.ones[:, 0:C], T.ones[:, 0:C], -1.0, ALU.mult, ALU.add, ["ones"], ["ramp"])
     ts(T.pi[:, 1:2], p0, 3, None, ALU.bitwise_and, None, ["pi0"], ["pi1"])
     ts(T.pi[:, 2:3], p0, 2, 3, ALU.logical_shift_right, ALU.bitwise_and, ["pi0"], ["pi2"])
-    tt(T.pi[:, 6:7], p0, T.pi[:, 5:6], ALU.add, ["pi0", "pi5"], ["pi6"])
-    ts(T.pi[:, 3:4], p0, 15, None, ALU.bitwise_and, None, ["pi0"], ["pi3"])
-    ts(T.pi[:, 4:5], p0, 31, None, ALU.bitwise_and, None, ["pi0"], ["pi4"])
-    ts(T.pi[:, 7:8], T.pi[:, 6:7], 7, None, ALU.bitwise_and, None, ["pi6"], ["pi7"])
-    fill(T.inv[:], 0.0, ["inv"])
-    cp(T.pf[:], T.pi[:], ["pi%d" % i for i in range(8)], ["pf"])
-    afill(T.b0[:], 1, ["b0", "b0a", "b0b"])
-    afill(T.b1[:], 0, ["b1"])
-    afill(T.fw[:, 0:1], 0, ["fw0"])
-    afill(T.c8[:, 0:7], -100, ["c8a"])
-    afill(T.c8[:, 7:8], 0, ["c8b"])
-    afill(T.Rr[:, 96:128], 0, ["Rrt"])
-    act(T.cf[:, 1:2], T.pf[:, 3:4], ACT.Identity, ["pf"], ["cf1"], scale=16.0)
-
-    def offsets(src, lo, n, r, w):
-        ts(T.O[:, lo:lo + n], src, 4.0, tcol, ALU.mult, ALU.add, r + ["pf"], [w])
+    cp(T.pf[:, 1:3], T.pi[:, 1:3], ["pi1", "pi2"], ["pf"])
+    for i in range(2):
+        afill(T.inv[:, C * i:C * i + C], 0, ["inv%d" % i])
 
     def engine_sets(t, src, dst):
         e = topo.engines(src, dst)
         return (e[:len(e) // 2], e[len(e) // 2:]) if t == 0 else (e, e)
 
-    def operands_and_send(t):
-        keys = file_keys(t)
-        for i in range(4):
-            act(T.Bt[:, A * i:A * i + A], window(t).indirect(T.O[:, 10 * i:10 * i + 10]), ACT.Copy, keys + ["O0"], ["Bt%d" % i])
-        for i in range(4):
-            tt(T.Z[:, A * i:A * i + A], window(t).indirect(T.O[:, 40 + 10 * i:50 + 10 * i]), T.Bt[:, A * i:A * i + A], ALU.add,
-               keys + ["O1", "Bt%d" % i], ["Z%d" % i])
-        quant(T["zq%d" % t][:], T["zp%d" % t][:], T.Z[:], quarters("Z"), ["zq%d" % t])
+    def send(t):
+        quant(T["zq%d" % t][:], T["zp%d" % t][:], T.Z[:], ["Z%d" % i for i in range(5)], ["zq%d" % t])
         peer = T.cores[rank ^ STEP[t]]
         rid, pid = topo.addr(peer)[0:2]
         sides = ((T["gq%d" % t][:].bitcast(dt.uint8), T["zq%d" % t][:].bitcast(dt.uint8)), (T["gp%d" % t][:], T["zp%d" % t][:]))
@@ -238,33 +224,50 @@ def rank_program(g, core, T, topo):
                         "fn": lambda out=out, in_=in_, mask=mask: g.remote_dma(out, in_, T.sem["arr%d" % t], T.sem.sent, pid, rid, mask)})
         ops.append({"q": None, "r": [], "w": ["gq%d" % t], "sem": "arr%d" % t, "inc": sum(len(es) for es in engine_sets(t, peer, core))})
 
-    def renamers(t):
-        lo = C + A * t
-        cp(T.inv[:].indirect(ld(t)), T.ramp[:, lo:lo + A], ["ramp2", "ldu"], ["inv"])
+    def operands(t, shadow):
+        keys = file_keys(t)
+        for e in range(4):
+            acp(T.Bt[:, A * e:A * e + A], window(t).indirect(T.O[:, 24 * e:24 * e + 10]), keys + ["O%d" % e],
+                ["Bt%d" % e] + (["Bt4"] if e == 3 else []))
+        shadow()
+        for e in range(4):
+            tt(T.Z[:, e:4 * A:4], window(t).indirect(T.O[:, 24 * e + 10:24 * e + 20]), T.Bt[:, A * e:A * e + A],
+               ALU.add, keys + ["O%d" % e, "Bt%d" % e], ["Z%d" % e] + (["Z4"] if e == 3 else []))
 
-    def renamers_of_operands(t):
-        act(T.krep[:, 0:A], T.inv[:].indirect(lb(t)), ACT.Copy, ["inv", "lbu"], ["krepb"])
-        act(T.krep[:, A:2 * A], T.inv[:].indirect(la(t)), ACT.Copy, ["inv", "lau"], ["krepa"])
+    def deal(name, src, n, r):
+        for h in range(2):
+            dma("S", "dc%s%d" % (name, h), T["crs" + name][:, n * h:n * h + n], src[16 * h:128:32, :], r, ["crs%s%d" % (name, h)])
+        for h in range(2):
+            dma("S", "do%s%d" % (name, h), T["own" + name][:, n * h:n * h + n], src[0:128:16, 16 * n * h:16 * n * (h + 1)], r, ["own%s%d" % (name, h)])
 
-    def to_list(t, src, r):
-        act(T["ro%d" % t][:], src.indirect(T.RL[:]), ACT.Copy, r + ["RL0", "RL1", "RL2"], ["ro%d" % t])
-        dma("S", "dk%d" % t, T["kl%d" % t][:], T["ro%d" % t][0:128:16, :], ["ro%d" % t], ["kl%d" % t])
+    own = lambda name: ["own%s0" % name, "own%s1" % name]
 
-    def slots(out, src, n, r, w):
-        scan(out, T.d0n[:, 0:n], src[:, 0:n], 0.0, ALU.mult, ALU.add, r + ["d0n"], w)
+    def crossed(out, name, n, k, tab, add=0.0):
+        for q in range(2):
+            ts(T[out][:, q:2 * n:2], T["crs" + name][:, n * k * q + tab:n * k * (q + 1):k], add, None, ALU.add, None,
+               ["crs%s%d" % (name, q)], [out + str(q)])
 
-    kp = lambda t: T.kp[:, t:t + 1]
-    keep = lambda t: T.r8[:, 8 * t + 7:8 * t + 8]
+    def lookup(ro, k, tab, win, lists, r, add=0.0):
+        for h in range(2):
+            aff(T[ro][:, A * k * h + tab:A * k * (h + 1):k], win.indirect(lists[h]), 1.0, add, r, ["%s%d%d" % (ro, tab, h)])
 
-    def commit(t):
-        lo = C + A * t
-        tt(T.wk[:], T.fw[:, 1:A + 1], T.ramp[:, lo:lo + A], ALU.min, ["fw", "ramp2"], ["wk"])
-        ts(kp(t), keep(t), 1.0, None, ALU.min, None, ["r8%d" % t], ["kp%d" % t])
-        cp(T["C%d" % t][:].indirect(ld(t)), T.wk[:], ["wk", "ldu"], ["C%d" % t])
+    AT = {"D0": 0, "D1": 120, "D3": 240, "D0p": 360, "D0q": 480, "cm": 600, "b1": 648}
+    D = lambda d, a, b, s=1: T.DD[:, AT[d] + a:AT[d] + b:s]
+    keep = lambda t: T.k8[:, 8:9] if t == 2 else D("D%d" % t, 26, 27)
+    signs = lambda t: T.sg[:, 176 * t:176 * t + A + 1]
 
-    def after_arrival(t, a1=None, a2=None, v1=None):
-        gq, gp, n = T["gq%d" % t][:], T["gp%d" % t][:], (C if t == R - 1 else 2 * A)
-        h = n // 2
+    def choose(out, d0, d1, n, turned, r, w, alu=ALU.max):
+        x = 0 if n == 20 else 2
+        cp(D(d0, 25, 120, 3), T[turned][:, 0:16 * n].indirect(T.XL[:, x:x + 2]), r + ["XL%d" % x, "XL%d" % (x + 1), "DD"], [d0 + "e"])
+        scan(T[out][:, 0:3 * n], D(d0, 24, 24 + 3 * n), T[d1][:, 0:3 * n], 0.0, ALU.mult, alu,
+             ["DD", d0 + "e", d0 + "k"] + (own("1") if d1 == "own1" else [d1 + "a", d1 + "b", d1 + "c"]), w)
+
+    def keep_in(d0, t, n):
+        ts(D(d0, 26, 26 + 3 * n, 3), T.ones[:, 0:n], keep(t), 0.0, ALU.mult, ALU.max, ["ones", "DD", "D%dk" % t], [d0 + "k"])
+
+    def after_arrival(t, v1):
+        gq, gp, n = T["gq%d" % t][:], T["gp%d" % t][:], (24 if t == R - 1 else 20)
+        KX, win = T["KX%d" % t], signs(t)
         for b in range(4):
             mm(b, A, T.wq[:, 128 * b:128 * b + 128], T.wp[:, 128 * b:128 * b + 128], gq, gp, ["wq", "wp", "gq%d" % t])
         for b in range(4):
@@ -273,182 +276,193 @@ def rank_program(g, core, T, topo):
                 ts(T.H[:, b:4 * A:4], bank, 0.0, 0.015625, ALU.max, ALU.mult, [], ["H%d" % b, "ps%d" % b])
             else:
                 act(T.H[:, b:4 * A:4], bank, ACT.Relu, [], ["H%d" % b, "ps%d" % b], scale=0.015625)
-        if a1:
-            a1()
         quant(T.hq[:], T.hp[:], T.H[:], quarters("H"), ["hq"])
-        if v1:
-            v1()
-        mm(5, A, T.u2q[:, 128:256], T.u2p[:, 128:256], T.hq[:], T.hp[:], ["u2q", "u2p", "hq"])
-        mm(4, A, T.u2q[:, 0:128], T.u2p[:, 0:128], T.hq[:], T.hp[:], ["u2q", "u2p", "hq"])
+        v1()
+        mm(5, A, T.u2q[:], T.u2p[:], T.hq[:], T.hp[:], ["u2q", "u2p", "hq"])
         for b in range(4):
             mm(b, A, T.eq[:, 128 * b:128 * b + 128], T.ep[:, 128 * b:128 * b + 128], T.hq[:], T.hp[:], ["eq%d" % b, "hq"])
-        KO = T["KO%d" % t]
-        ts(KO[:, 0:n // 16], T["kl%d" % t][:, 0:n // 16], float(1 - C - A * t), 0.0, ALU.add, ALU.max, ["kl%d" % t], ["KO"])
-        act(T.sg[:], T.ps5[:, 0:A], ACT.Sign, [], ["key", "ps5"], scale=2.0 ** 32, bias=2.0 ** -120, accum_out=T.key[:, 0:1])
+        act(T.sg[:, 176 * t + 1:176 * t + A + 1], T.ps5[:, 0:A], ACT.Sign, [], ["key", "sg%d" % t, "ps5"],
+            scale=2.0 ** 32, bias=2.0 ** -120, accum_out=T.key[:, 0:1])
+        keys = ["sg%d" % t, "sgc", "KX%d0" % t, "KX%d1" % t]
+        c = 6
+        acp(T.Rc[:, 16 * c:16 * n], win.indirect(KX[:, c:n]), keys, ["Rc1"])
         lo = 4 * (C + A * t)
         for b in range(4):
-            act(T.F[:, lo + b:lo + 4 * A:4], T["ps%d" % b][:, 0:A], ACT.Copy, [], ["F%d%d" % (t, b), "ps%d" % b])
-        if a2:
-            a2()
-        ts(T.fw[:, 1:A + 1], T.ps4[:, 0:A], 0.0, 1024.0, ALU.is_ge, ALU.mult, [], ["fw", "ps4"])
-        cuts = [0, 4 if n < C else 6, n // 32, n // 32 + 6, n // 16]
+            acp(T.F[:, lo + b:lo + 4 * A:4], T["ps%d" % b][:, 0:A], [], ["F%d%d" % (t, b), "ps%d" % b])
+        scan(T.bc[:], T.b0[:], D("b1", 0, 32), T.key[:, 0:1], ALU.mult, ALU.add, ["b0", "b0a", "b0b", "b1", "key"], ["bc"])
+        cp(T.Rc[:, 0:16 * c], win.indirect(KX[:, 0:c]), keys, ["Rc0"])
+        turn(T.tr[:], T.bc[:], ["bc"], ["tr"])
+        turn(T.Tc[:, 0:16 * c], T.Rc[:, 0:16 * c], ["Rc0"], ["Tc0"])
+        ts(D("cm", 0, 8), T.tr[:, 0:8], T.tr[:, 8:9], T.tr[:, 9:10], ALU.subtract, ALU.is_gt, ["tr", "DD"], ["cm"])
+        turn(T.Tc[:, 16 * c:16 * n], T.Rc[:, 16 * c:16 * n], ["Rc1"], ["Tc1"])
+        last = t == R - 1
+        m = 9 if last else 28
+        scan(T.k8[:, 0:m] if last else D("D%d" % t, 2, 3 * m, 3), D("cm", 0, m), T.ones[:, 0:m], -1.0, ALU.add, ALU.min,
+             ["cm", "DD", "ones"], ["D%dk" % t])
+        if last:
+            keep_in("D3", t, n)
+            choose("Xc", "D3", "D21", n, "Tc", ["Tc0", "Tc1"], ["Xc"], ALU.add)
+        else:
+            choose("Xc", "D%d" % t, ("own1", "D11")[t], n, "Tc", ["Tc0", "Tc1"], ["Xc"])
+        for e in ((0, 2, 1, 3) if last else range(4)):
+            ts(T.O[:, 24 * e:24 * e + n], T.Xc[:, 2:3 * n:3], 2.0 if last else 4.0, float(e), ALU.mult, ALU.add, ["Xc"], ["O%d" % e])
 
-        def flags(i):
-            a, b = cuts[i], cuts[i + 1]
-            tt(T.P[:, 32 * a:32 * b:2], T.fw[:, 0:A + 1].indirect(KO[:, a:b]), T.Pk[:, 16 * a:16 * b],
-               ALU.min, ["fw", "fw0", "KO"] + quarters("Pk"), ["f%d" % i])
-        scan(T.bc[:], T.b0[:], T.b1[:], T.key[:, 0:1], ALU.mult, ALU.add, ["b0", "b0a", "b0b", "b1", "key"], ["bc"])
-        flags(0)
-        op("V", lambda: V.transpose(T.tr[:], T.bc[:]), ["bc"], ["tr"])
-        flags(1)
-        ts(T.cm[:], T.tr[:, 0:8], T.tr[:, 8:9], T.tr[:, 9:10], ALU.subtract, ALU.is_gt, ["tr"], ["cm"])
-        flags(2)
-        scan(T.r8[:, 8 * t:8 * t + 8], T.cm[:], T.c8[:], -1.0, ALU.add, ALU.max, ["cm", "c8a", "c8b"], ["r8%d" % t])
-        flags(3)
-        ts(T.d0h[:, 7:2 * n:8], T.d0n[:, 1:n:4], keep(t), None, ALU.min, None, ["d0n", "r8%d" % t], ["keep"])
-        if t == R - 1:
-            ts(T.P[:, 7:2 * n:8], T.rbs[:], keep(t), 1024.0, ALU.subtract, ALU.mult, ["rbs", "r8%d" % t], ["h3"])
-        for i in range(2):
-            a, b = 2 * h * i, 2 * h * (i + 1)
-            scan(T.XO[:, a:b], T.d0h[:, a:b], T.P[:, a:b], 0.0, ALU.mult, ALU.max,
-                 ["d0h", "keep", "h0", "h1", "h2", "h3", "f%d" % (2 * i), "f%d" % (2 * i + 1)], ["XO%d" % i])
-            offsets(T.XO[:, a + 7:b:8], i * h // 4, h // 4, ["XO%d" % i], "O%d" % i)
-
-    HS = ["h0", "h1", "h2", "h3"]
     MK = ["M0a", "M0b"]
+    L90, n90 = T.lst[:, LB:LB + 90], ["la", "lb", "ld"]
     cp(T.lu[:, LM:LM + 24], T.lst[:, LM:LM + 24], ["m"], ["mu"])
-    ts(T.mask4[:], T.em4[:], qcol, None, ALU.is_equal, None, ["em4", "pf"], ["mask4"])
-    act(T.M0[:, A:C], T.ramp[:, 0:C].indirect(T.lu[:, 10:24]), ACT.Copy, ["ramp", "mu"], ["M0b"])
-    cp(T.M0[:, 0:A], T.ramp[:, 0:C].indirect(T.lu[:, 0:10]), ["ramp", "mu"], ["M0a"])
-    cp(T.lu[:, LA:LD], T.lst[:, LA:LD], ["la", "lb"], ["lau", "lbu"])
-    tt(T.Pn[:, 0:A], M0.indirect(lb(0)), T.mask4[:], ALU.mult, MK + ["lbu", "mask4"], ["Pn0"])
-    ts(T.cf[:, 2:3], T.pf[:, 3:4], 8.0, float(1 - C), ALU.is_ge, ALU.mult, ["pf"], ["cf2"])
-    slots(T.Xn[:, 0:A], T.Pn, A, ["Pn0"], ["Xn0"])
-    cp(T.lu[:, LD:LD + 30], T.lst[:, LD:LD + 30], ["ld"], ["ldu"])
-    offsets(T.Xn[:, 3:A:4], 0, 40, ["Xn0"], "O0")
-    tt(T.Pn[:, A:2 * A], M0.indirect(la(0)), T.mask4[:], ALU.mult, MK + ["lau", "mask4"], ["Pn1"])
+    ts(T.mask4[:], T.em[:], 1.0 / 512, qcol, ALU.mult, ALU.is_equal, ["em", "pf"], ["mask4"])
+    ts(T.pi[:, 4:5], p0, 4, 1, ALU.logical_shift_right, ALU.bitwise_and, ["pi0"], ["pi4"])
+    acp(T.M0[:, 192:C], ramp.indirect(T.lu[:, 12:24]), ["ramp", "mu"], ["M0b"])
+    afill(T.inv[:, 2 * C:3 * C], 0, ["inv2"])
+    afill(T.b0[:], 1, ["b0", "b0a", "b0b"])
+    afill(T.sg[:, 0:R * 176:176], -1, ["sgc"])
+    cp(T.M0[:, 0:192], ramp.indirect(T.lu[:, 0:12]), ["ramp", "mu"], ["M0a"])
+    cp(T.lu[:, LB:LD], T.lst[:, LB:LD], ["la", "lb"], ["lu"])
+    ts(T.pi[:, 5:6], p0, 15, None, ALU.bitwise_and, None, ["pi0"], ["pi5"])
+    tt(T.Pn[:, 0:A], M0.indirect(lb(0)), T.mask4[:], ALU.mult, MK + ["lu", "mask4"], ["Pn0"])
+    tt(T.Pn[:, A:2 * A], M0.indirect(la(0)), T.mask4[:], ALU.mult, MK + ["lu", "mask4"], ["Pn1"])
+    scan(T.Xn[:, 0:A], T.em[:], T.Pn[:, 0:A], 0.0, ALU.min, ALU.max, ["em", "Pn0"], ["Xn0"])
+    ts(T.ln[:, 0:90], L90, 31, None, ALU.bitwise_and, None, n90, ["ln"])
+    ts(T.O0[:, 0:40], T.Xn[:, 3:A:4], 4.0, tcol, ALU.mult, ALU.add, ["Xn0", "pf"], ["O00"])
+    scan(T.Xn[:, A:2 * A], T.em[:], T.Pn[:, A:2 * A], 0.0, ALU.min, ALU.max, ["em", "Pn1"], ["Xn1"])
+    ts(T.rb[:, 0:90], T.ln[:, 0:90], 383.0, None, ALU.mult, None, ["ln"], ["rb"])
+    ts(T.O0[:, 40:80], T.Xn[:, A + 3:2 * A:4], 4.0, tcol, ALU.mult, ALU.add, ["Xn1", "pf"], ["O01"])
+    ts(T.pi[:, 6:7], p0, 4, 6, ALU.logical_shift_right, ALU.bitwise_and, ["pi0"], ["pi6"])
+    ts(T.pi[:, 3:4], p0, 31, None, ALU.bitwise_and, None, ["pi0"], ["pi3"])
+    cuts = [0, 6, 16, 26, 34, 40]
+    for i in range(5):
+        a, b = cuts[i], cuts[i + 1]
+        acp(T.Bt[:, 16 * a:16 * b], window(0).indirect(T.O0[:, a:b]), ["x", "O00"], ["Bt%d" % i])
+    for i in range(5):
+        a, b = cuts[i], cuts[i + 1]
+        tt(T.Z[:, 16 * a:16 * b], window(0).indirect(T.O0[:, 40 + a:40 + b]), T.Bt[:, 16 * a:16 * b], ALU.add, ["x", "O01", "Bt%d" % i], ["Z%d" % i])
+    send(0)
+
+    iota(T.true[:, C:C + A], [[1, A]], C, 0, ["true0"])
+    iota(T.true[:, C + A:C + 3 * A], [[A, 2], [1, 10], [10, 16]], C + A, 0, ["true1"])
+    lookup("ro1", 3, 1, M0, (lb(1), la(1)), MK + ["lu"])
+    lookup("ro1", 3, 2, M0, (lb(1), la(1)), MK + ["lu"])
+    lookup("ro2", 2, 1, M0, (lb(2), la(2)), MK + ["lu"])
+    tt(T.ra[:, 0:90], T.rb[:, 0:90], L90, ALU.add, ["rb"] + n90, ["ra"])
+    tt(T.pi[:, 7:8], p0, T.pi[:, 6:7], ALU.add, ["pi0", "pi6"], ["pi7"])
+    ts(T.k0[:, 0:70], T.ra[:, 0:70], 3.0 / 32, None, ALU.mult, None, ["ra"], ["k0"])
     ts(T.u2j[:], T.u2i[:], 7, None, ALU.bitwise_and, None, ["u2i"], ["u2j"])
-    scan(T.Xn[:, A:2 * A], T.d0n[:, 0:A], T.Pn[:, A:2 * A], 0.0, ALU.mult, ALU.add, ["d0n", "Pn1"], ["Xn1"])
-    ts(T.UL[:, 0:8], T.ramp[:, 0:8], 16.0, None, ALU.mult, None, ["ramp"], ["ULa"])
-    offsets(T.Xn[:, A + 3:2 * A:4], 40, 40, ["Xn1"], "O1")
-    renamers(0)
-
-    def first_places(l, key, lo):
-        act(T.rbg[:, lo:lo + A], M0.indirect(l), ACT.Copy, MK + [key], ["rb%d" % lo])
-    first_places(lb(1), "lbu", 0)
-    first_places(la(1), "lau", A)
-    operands_and_send(0)
-
-    RB = ["rb0", "rb%d" % A]
-    iota(T.C0[:], [[0, C]], 0, 0, ["C0"])
-    iota(T.C1[:], [[0, C]], 0, 0, ["C1"])
-    renamers_of_operands(1)
-    afill(T.krep[:, 2 * A:C], 0, ["krept"])
-    ts(T.RL[:, 0:24:3], T.ramp[:, 0:16:2], T.cf[:, 1:2], None, ALU.add, None, ["ramp", "cf1"], ["RL0"])
-    ts(T.RL[:, 2:24:3], T.ramp[:, 129:145:2], T.cf[:, 1:2], None, ALU.add, None, ["ramp", "cf1"], ["RL2"])
-    ts(T.RL[:, 1:24:3], T.ramp[:, 256:272:2], T.cf[:, 1:2], T.cf[:, 2:3], ALU.add, ALU.add, ["ramp", "cf1", "cf2"], ["RL1"])
-    ts(T.UL[:, 8:16], T.u2j[:], 16.0, None, ALU.mult, None, ["u2j"], ["ULb"])
-    to_list(0, T.krep[:], ["krepa", "krepb", "krept"])
-    dma("S", "dv", T.vt[:], T.v[:], ["gq0"], ["vt"])
+    cp(T.inv[:].indirect(T.k0[:, 60:70]), T.true[:, 1:A + 1], ["ramp", "k0"], ["inv", "inv0", "inv1", "inv2"])
+    ts(T.pi[:, 6:7], T.pi[:, 7:8], 7, None, ALU.bitwise_and, None, ["pi7"], ["pi6"])
+    ts(T.UL[:], T.u2j[:], 16.0, None, ALU.mult, None, ["u2j"], ["UL"])
     quant(T.uq[:], T.up[:], T.ut[:], ["ut"], ["uq"])
-    fill(T.d0h[:, 0:2 * C:8], 0.0, ["d0h"])
-    cp(T.u2q[:].bitcast(dt.uint32), T.uq[:].bitcast(dt.uint32).indirect(T.UL[:]), ["uq", "ULa", "ULb"], ["u2q"])
-    mask_by_quarter(T.mk, T.rbg, 2 * A, RB, "mk")
-    act(T.cf[:, 4:5], T.pf[:, 7:8], ACT.Identity, ["pf"], ["cf4"], scale=-0.125, bias=A / 2 + 0.875)
-    act(T.u2p[:], T.up[:].indirect(T.UL[:]), ACT.Copy, ["uq", "ULa", "ULb"], ["u2p"])
-    act(T.cf[:, 3:4], qcol, ACT.Identity, ["pf"], ["cf3"], scale=8.0, bias=tcol)
-    ts(T.cf[:, 5:6], T.pf[:, 4:5], 9.0, 4095.0, ALU.is_equal, ALU.mult, ["pf"], ["cf5"])
-    tt(T.Pk[:, 0:A], T.krep[:, 0:A], T.mask4[:], ALU.mult, ["krepb", "mask4"], ["Pk0", "Pk1"])
-    ts(T.b0[:, 16:17], T.pf[:, 4:5], 8.0, T.cf[:, 5:6], ALU.not_equal, ALU.add, ["pf", "cf5"], ["b0b"])
+    cp(T.pf[:, 3:7], T.pi[:, 3:7], ["pi3", "pi4", "pi5", "pi6"], ["pf2"])
+    cp(T.u2q[:].bitcast(dt.uint32), T.uq[:].bitcast(dt.uint32).indirect(T.UL[:]), ["uq", "UL"], ["u2q"])
+    ts(T.cf[:, 5:6], run, 9.0, 4095.0, ALU.is_equal, ALU.mult, ["pf2"], ["cf5"])
+    lookup("ro1", 3, 0, T.inv[:], (T.k0[:, 10:20], T.k0[:, 40:50]), ["inv", "k0"], base(0))
+    deal("1", T.ro1, 30, ["ro1%d%d" % (k, h) for k in range(3) for h in range(2)])
+    aff(T.cf[:, 4:5], row, -0.125, A / 2 + 0.875, ["pf2"], ["cf4"])
+    aff(T.cf[:, 0:1], lane, 32.0, half, ["pf2"], ["cf0"])
+    acp(T.u2p[:], T.up[:].indirect(T.UL[:]), ["uq", "UL"], ["u2p"])
+    lookup("ro2", 2, 0, T.inv[:], (T.k0[:, 20:30], T.k0[:, 50:60]), ["inv", "k0"], base(0))
+    deal("2", T.ro2, 20, ["ro2%d%d" % (k, h) for k in range(2) for h in range(2)])
+    ts(T.b0[:, 16:17], run, 8.0, T.cf[:, 5:6], ALU.not_equal, ALU.add, ["pf2", "cf5"], ["b0b"])
     ts(T.b0[:, 0:1], T.cf[:, 5:6], -4096.0, 1.0 / 8192, ALU.add, ALU.mult, ["cf5"], ["b0a"])
-    tt(T.Pk[:, A:2 * A], T.krep[:, A:2 * A], T.mask4[:], ALU.mult, ["krepa", "mask4"], ["Pk2", "Pk3"])
+    ts(T.cf[:, 1:2], lane, 10.0, -304.0, ALU.is_ge, ALU.mult, ["pf2"], ["cf1"])
     for b in range(4):
         quant(T.eq[:, 128 * b:128 * b + 128], T.ep[:, 128 * b:128 * b + 128], T.eb[:, 3 - b:515 - b], ["eb"], ["eq%d" % b])
-    slots(T.P[:, 1:4 * A:2], T.mk, 2 * A, quarters("mk"), HS)
-    ts(T.b1[:, 0:1], T.cf[:, 4:5], T.b0[:, 0:1], -2.0, ALU.mult, ALU.mult, ["cf4", "b0a"], ["b1"])
-    after_arrival(0, lambda: first_places(lb(2), "lbu", 0), lambda: first_places(la(2), "lau", A))
-    operands_and_send(1)
+    ts(D("b1", 0, 1), T.cf[:, 4:5], T.b0[:, 0:1], -2.0, ALU.mult, ALU.mult, ["cf4", "b0a", "DD"], ["b1"])
+    ts(T.k1[:, 0:90], T.ra[:, 0:90], 3.0 / 32, 1.0, ALU.mult, ALU.add, ["ra"], ["k1"])
+    ts(T.XL[:, 0:1], T.cf[:, 0:1], T.cf[:, 1:2], None, ALU.add, None, ["cf0", "cf1"], ["XL0"])
+    ts(T.XL[:, 1:2], T.cf[:, 0:1], 208.0, 319.0, ALU.add, ALU.min, ["cf0"], ["XL1"])
+    dma("S", "dv", T.vt[:], T.v[:], ["gq0"], ["vt"])
 
-    mask_by_quarter(T.mk, T.rbg, 2 * A, RB, "mk")
-    renamers(1)
-    renamers_of_operands(2)
-    to_list(1, T.krep[:], ["krepa", "krepb", "krept"])
-    commit(0)
-    mask_by_quarter(T.Pk, T.krep, 2 * A, ["krepa", "krepb"], "Pk")
-    slots(T.P[:, 1:4 * A:2], T.mk, 2 * A, quarters("mk"), HS)
-    for i, (l, key) in enumerate(((lb(2), "lbu"), (la(2), "lau"))):
-        tt(T.Pn[:, A * i:A * i + A], T.C0[:].indirect(l), T.mask4[:], ALU.mult, ["C0", key, "mask4"], ["Pn%d" % i])
+    def gap0():
+        crossed("KX0", "1", 10, 3, 0, -base(0))
+        cp(T.inv[:].indirect(T.k1[:, 70:80]), T.pp[:], ["pp", "k1"], ["inv"])
+    after_arrival(0, gap0)
+    operands(1, lambda: crossed("KP0", "2", 10, 2, 0, -base(0)))
+    send(1)
 
-    def round0_places():
-        slots(T.Xn[:], T.Pn, 2 * A, ["Pn0", "Pn1"], ["Xn0", "Xn1"])
-        ts(T.OL[:], T.ramp[:, 0:8:4], T.cf[:, 3:4], 4.0, ALU.add, ALU.mult, ["ramp", "cf3"], ["OL"])
-        ts(T.P[:, 1:4 * A:8], T.Xn[:, 3:2 * A:4], kp(0), None, ALU.mult, None, ["Xn0", "Xn1", "kp0"], ["h0"])
-    after_arrival(1, lambda: mask_by_quarter(T.mk, T.M0, C, MK, "mk", (0, 1)),
-                  lambda: mask_by_quarter(T.mk, T.M0, C, MK, "mk", (2, 3)), round0_places)
-    operands_and_send(2)
+    lookup("ro3", 1, 0, T.inv[:], (T.k1[:, 20:30], T.k1[:, 50:60]), ["inv", "k1"], base(1))
+    acp(T.Rp[:, 0:2 * A], signs(0).indirect(T.KP0[:, 0:20]), ["sg0", "sgc", "KP00", "KP01"], ["Rp"])
+    ts(T.k2[:, 0:10], T.ra[:, 80:90], 3.0 / 32, 2.0, ALU.mult, ALU.add, ["ra"], ["k2"])
+    cp(T.inv[:].indirect(T.k2[:, 0:10]), T.pp[:], ["pp", "k2"], ["inv"])
+    deal("3", T.ro3, 10, ["ro300", "ro301", "inv"])
+    deal("A", T.inv, 36, ["inv"])
+    turn(T.Tp[:, 0:2 * A], T.Rp[:, 0:2 * A], ["Rp"], ["Tp"])
+    quant(T.vq[:], T.vp[:], T.vt[:], ["vt"], ["vq"])
+    acp(T.Dp[:, 0:60:3], T.own2[:, 0:40:2], own("2"), ["Dpa"])
+    acp(T.Dp[:, 1:60:3], T.own2[:, 1:40:2], own("2"), ["Dpb"])
+    acp(T.Dp[:, 2:60:3], T.own2[:, 1:40:2], own("2"), ["Dpc"])
+    aff(T.cf[:, 2:3], lane, 16.0, half, ["pf2"], ["cf2"])
+    acp(T.D11[:, 2:60:3], T.own2[:, 1:40:2], own("2"), ["D11c"])
+    choose("Xp", "D0", "Dp", 20, "Tp", ["Tp"], ["Xp"])
+    cp(T.XL[:, 2:3], T.cf[:, 2:3], ["cf2"], ["XL2"])
+    ts(T.XL[:, 3:4], T.cf[:, 2:3], 256.0, 383.0, ALU.add, ALU.min, ["cf2"], ["XL3"])
+    acp(T.D11[:, 1:60:3], T.Xp[:, 2:60:3], ["Xp"], ["D11b"])
 
-    mask_by_quarter(T.mk2, T.C0, C, ["C0"], "mkb")
-    renamers(2)
-    to_list(2, T.inv[:], ["inv"])
-    commit(1)
-    mask_by_quarter(T.Pk, T.inv, C, ["inv"], "Pk", (0, 1))
-    mask_by_quarter(T.mk3, T.C1, C, ["C1"], "mkc")
-    slots(T.Xh[:], T.mk, C, quarters("mk"), ["Xh"])
-    slots(T.XO[:, 0:C], T.mk2, C, quarters("mkb"), ["XO0", "XO1"])
-    cp(T.m0s[:], T.Xh[:, 3:C:4], ["Xh"], ["m0s"])
-    ts(T.c0s[:], T.XO[:, 3:C:4], kp(0), None, ALU.mult, None, ["XO0", "XO1", "kp0"], ["c0s"])
-    cp(T.P[:, 5:2 * C:8], T.Xh[:, 3:C:4], ["Xh"], ["h2"])
-    tt(T.rbs[:], T.c0s[:], T.m0s[:], ALU.max, ["c0s", "m0s"], ["rbs"])
-    ts(T.P[:, 3:2 * C:8], T.XO[:, 3:C:4], kp(0), kp(1), ALU.mult, ALU.mult, ["XO0", "XO1", "kp0", "kp1"], ["h1"])
-    ts(T.rbs[:], T.rbs[:], 1.0 / 1024, None, ALU.mult, None, ["rbs"], ["rbs"])
+    def gap1():
+        crossed("KX1", "3", 10, 1, 0, -base(1))
+        cp(T.D11[:, 0:60:3], T.own3[:], own("3"), ["D11a"])
+    after_arrival(1, gap1)
+    operands(2, lambda: crossed("KP1", "A", 12, 3, 0))
+    send(2)
 
-    def round1_places():
-        slots(T.Xh[:], T.mk3, C, quarters("mkc"), ["Xh"])
-        ts(T.P[:, 1:2 * C:8], T.Xh[:, 3:C:4], kp(1), None, ALU.mult, None, ["Xh", "kp1"], ["h0"])
-    after_arrival(2, lambda: mask_by_quarter(T.Pk, T.inv, C, ["inv"], "Pk", (2, 3)), None, round1_places)
+    crossed("KP2", "A", 12, 3, 1)
+    crossed("KX2", "A", 12, 3, 2)
+    acp(T.Rp[:], signs(0).indirect(T.KP1[:]), ["sg0", "sgc", "KP10", "KP11"], ["Rp"])
+    acp(T.Rq[:], signs(1).indirect(T.KP2[:]), ["sg1", "sgc", "KP20", "KP21"], ["Rq"])
+    m24 = T.lst[:, LM:LM + 24]
+    for h in range(2):
+        ts(T.Dp[:, 3 * h:72:6], T.ownA[:, 36 * h:36 * h + 36:3], base(0), None, ALU.add, None, own("A"), ["Dpa" + "+" * h])
+    cp(T.Dp[:, 1:72:3], m24, ["m"], ["Dpb"])
+    cp(T.Dp[:, 2:72:3], m24, ["m"], ["Dpc"])
+    turn(T.Tp[:], T.Rp[:], ["Rp"], ["Tp"])
+    keep_in("D0p", 0, 24)
+    for h in range(2):
+        ts(T.Dq[:, 3 * h:72:6], T.ownA[:, 36 * h + 1:36 * h + 36:3], base(1), None, ALU.add, None, own("A"), ["Dqa" + "+" * h])
+    choose("Xp", "D0p", "Dp", 24, "Tp", ["Tp", "Dpa+"], ["Xp"])
+    turn(T.Tq[:], T.Rq[:], ["Rq"], ["Tq"])
+    keep_in("D0q", 1, 24)
+    cp(T.Dq[:, 2:72:3], m24, ["m"], ["Dqc"])
+    acp(T.Dq[:, 1:72:3], T.Xp[:, 2:72:3], ["Xp"], ["Dqb"])
+    aff(T.D21[:, 2:72:3], T.Xp[:, 2:72:3], 2.0, 0.0, ["Xp"], ["D21c"])
+    for h in range(2):
+        aff(T.w1[:, h:24:2], T.ownA[:, 36 * h + 2:36 * h + 36:3], 1.0, base(2), own("A"), ["w1" + "+" * h])
+    choose("Xq", "D0q", "Dq", 24, "Tq", ["Tq", "Dqa+"], ["Xq"])
+
+    def gap2():
+        tt(T.w2[:], T.w1[:], T.D21[:, 2:72:3], ALU.subtract, ["w1", "w1+", "D21c"], ["w2"])
+        tt(T.D21[:, 0:72:3], T.w1[:], T.Xq[:, 2:72:3], ALU.subtract, ["w1", "w1+", "Xq"], ["D21a"])
+        tt(T.D21[:, 1:72:3], T.w2[:], T.Xq[:, 2:72:3], ALU.add, ["w2", "Xq"], ["D21b"])
+    after_arrival(2, gap2)
 
     keys = file_keys(R)
 
-    def gather_a(a, b, r, w):
-        act(T.Tt[:, 16 * a:16 * b], window(R).indirect(T.O[:, a:b]), ACT.Copy, keys + r, [w])
+    def gather(q, e, a, b):
+        (acp if q == "A" else cp)(T.Tt[:, 64 * a + e:64 * b:4], window(R).indirect(T.O[:, 24 * e + a:24 * e + b]), keys + ["O%d" % e], ["T%d%d" % (e, a)])
 
-    def gather_v(a, b, r, w):
-        cp(T.Tt[:, 16 * a:16 * b], window(R).indirect(T.O[:, a:b]), keys + r, [w])
-
-    def piece(i, r):
-        a, b = 128 * i, 128 * i + 128
+    def piece(i, a, b, r):
         quant(T.tq[:, a:b], T.tp[:, a:b], T.Tt[:, 4 * a:4 * b], r, ["tq%d" % i])
-        mm(5 + i, 128, T.vq[:], T.vp[:], T.tq[:, a:b], T.tp[:, a:b], ["vq", "tq%d" % i])
+        mm(5 + i, b - a, T.vq[:], T.vp[:], T.tq[:, a:b], T.tp[:, a:b], ["vq", "tq%d" % i])
         dma("S", "outs", T.oc[:, 4 * a:4 * b], T.tq[:, a:b].bitcast(dt.uint8), ["tq%d" % i], [])
 
-    def y_out(q, i):
-        a, b = 128 * i, 128 * i + 128
+    def y_out(i, a, b):
         bank = "ps%d" % (5 + i)
-        if q == "A":
-            act(T.ys[:, a:b], T[bank][:, 0:128], ACT.Copy, [], ["ys%d" % i, bank])
-        else:
-            cp(T.ys[:, a:b], T[bank][:, 0:128], [], ["ys%d" % i, bank])
-        dma(q, "outs", T.y[:, a:b], T.ys[:, a:b], ["ys%d" % i], [])
-    gather_a(0, 20, ["O0"], "Ta")
-    gather_v(20, 32, ["O0"], "Tb")
-    gather_a(32, 64, ["O0", "O1"], "Tc")
-    quant(T.vq[:], T.vp[:], T.vt[:], ["vt"], ["vq"])
-    piece(0, ["Ta", "Tb"])
-    gather_v(64, 80, ["O1"], "Td")
-    gather_a(80, 96, ["O1"], "Te")
-    y_out("S", 0)
-    piece(1, ["Tc"])
-    for b in range(3):
-        cp(T.Rr[:, 32 * b:32 * b + 32], T.XO[:, 8 * b + 7:2 * C:24], ["XO0", "XO1"], ["Rr%d" % b])
-    piece(2, ["Td", "Te"])
-    y_out("A", 1)
-    op("V", lambda: V.transpose(T.Rt[:], T.Rr[:]), ["Rr0", "Rr1", "Rr2", "Rrt"], ["Rt"])
-    y_out("S", 2)
-    cp(T.omc[:], T.Rt[:].indirect(T.OL[:]), ["Rt", "OL"], ["omc"])
+        cp(T.ys[:, a:b], T[bank][:, 0:b - a], [], ["ys%d" % i, bank])
+        dma("S", "outs", T.y[:, a:b], T.ys[:, a:b], ["ys%d" % i], [])
+    gather("A", 0, 0, 16)
+    ts(T.O[:, 96:120], T.Xc[:, 2:72:3], 0.5, None, ALU.mult, None, ["Xc"], ["O4"])
+    gather("V", 1, 0, 16)
+    gather("A", 2, 0, 16)
+    gather("V", 3, 0, 16)
+    for e in range(3):
+        gather("A", e, 16, 24)
+    piece(0, 0, 256, ["T%d0" % e for e in range(4)])
+    gather("V", 3, 16, 24)
+    piece(1, 256, C, ["T%d16" % e for e in range(4)])
+    acp(T.omr[:], T.true[:].indirect(T.O[:, 96:120]), ["ramp", "true0", "true1", "O4"], ["omr"])
+    dma("A", "outs", T.om[:], T.omr[0:128:16, :], ["omr"], [])
+    y_out(0, 0, 256)
+    y_out(1, 256, C)
     for k in range(4):
-        dma("A", "outs", T.osc[4 * k:4 * k + 4, :], T.tp[32 * k:32 * k + 4, :], ["tq0", "tq1", "tq2"], [])
-    for h in range(2):
-        dma("S", "outs", T.om[h:8:2, :], T.omc[:, 16 * h:16 * h + 12], ["omc"], [])
+        dma("A", "outs", T.osc[4 * k:4 * k + 4, :], T.tp[32 * k:32 * k + 4, :], ["tq0", "tq1"], [])
 
     count = emit(g, T, ops)
     g.wait_ge(T.sem.sent, count["sent"])

from concourse.mybir import dt, AluOpType, ActivationFunctionType

C, A, R = 384, 160, 3
STEP = [1, 2, 1]
HALF = "float16"


def _sb(n, d="float32"):
    return ("sbuf", [128, n], d)


SCRATCH = {
    "lst": _sb(128, "int32"), "lu": _sb(128, "uint16"),
    "F": _sb(4 * (C + R * A), "bfloat16"), "ut": _sb(512, "bfloat16"), "vt": _sb(512, "bfloat16"),
    "wq": _sb(512, "float8_e4m3fn_x4"), "wp": _sb(512, "uint8"),
    "uq": _sb(128, "float8_e4m3fn_x4"), "up": _sb(128, "uint8"),
    "u2q": _sb(128, "float8_e4m3fn_x4"), "u2p": _sb(128, "uint8"),
    "vq": _sb(128, "float8_e4m3fn_x4"), "vp": _sb(128, "uint8"),
    "eb": _sb(520, "bfloat16"), "eq": _sb(512, "float8_e4m3fn_x4"), "ep": _sb(512, "uint8"),
    "ones": _sb(520, "bfloat16"), "pp": _sb(A), "true": _sb(C + R * A),
    "pi": _sb(8, "int32"), "pf": _sb(8), "cf": _sb(8),
    "mask4": _sb(A, "bfloat16"), "u2i": _sb(8, "int32"), "u2j": _sb(8, "int32"), "UL": _sb(8, "uint16"), "XL": _sb(4, "uint16"),
    "b0": _sb(32), "k8": _sb(16), "key": _sb(2), "bc": _sb(32), "tr": _sb(32), "sg": _sb(R * 176, "bfloat16"),
    "em": _sb(A, "bfloat16"), "Pn": _sb(2 * A, HALF), "Xn": _sb(2 * A, HALF), "O0": _sb(80, "uint16"),
    "M0": _sb(C), "inv": _sb(3 * C, "bfloat16"),
    "ln": _sb(96, "int32"), "ra": _sb(96), "rb": _sb(96),
    "k0": _sb(72, "uint16"), "k1": _sb(96, "uint16"), "k2": _sb(16, "uint16"),
    "ro1": _sb(6 * A), "ro2": _sb(4 * A), "ro3": _sb(2 * A),
    "own1": _sb(60), "crs1": _sb(60), "own2": _sb(40), "crs2": _sb(40), "own3": _sb(20), "crs3": _sb(20),
    "ownA": _sb(72, "bfloat16"), "crsA": _sb(72, "bfloat16"),
    "Rc": _sb(C, "bfloat16"), "Tc": _sb(C, "bfloat16"), "Rp": _sb(C, "bfloat16"), "Tp": _sb(C, "bfloat16"),
    "Rq": _sb(C, "bfloat16"), "Tq": _sb(C, "bfloat16"),
    "DD": _sb(680), "Dp": _sb(72), "Dq": _sb(72), "D11": _sb(72), "D21": _sb(72),
    "Xc": _sb(72), "Xp": _sb(72), "Xq": _sb(72), "w1": _sb(24), "w2": _sb(24), "O": _sb(5 * 24, "uint16"),
    "Bt": _sb(4 * A, "bfloat16"), "Z": _sb(4 * A, "bfloat16"), "H": _sb(4 * A, "bfloat16"),
    "hq": _sb(A, "float8_e4m3fn_x4"), "hp": _sb(A, "uint8"),
    "Tt": _sb(4 * C, "bfloat16"), "tq": _sb(C, "float8_e4m3fn_x4"), "tp": _sb(C, "uint8"),
    "ys": _sb(C), "omr": _sb(C),
}
for _t in range(R):
    SCRATCH["zq%d" % _t] = _sb(A, "float8_e4m3fn_x4")
    SCRATCH["zp%d" % _t] = _sb(A, "uint8")
    SCRATCH["gq%d" % _t] = _sb(A, "float8_e4m3fn_x4")
    SCRATCH["gp%d" % _t] = _sb(A, "uint8")
    SCRATCH["KX%d" % _t] = _sb(24, "uint16")
    SCRATCH["KP%d" % _t] = _sb(24, "uint16")
for _b in range(8):
    SCRATCH["ps%d" % _b] = ("psum", [128, 512], "float32")

SEMAPHORES = (["cV", "cA", "cT", "cG", "sent", "outs", "arr0", "arr1", "arr2",
               "dm", "dla", "dlb", "dld", "dx", "du", "dv", "dwc", "dws"]
              + ["d%s%s%d" % (k, n, h) for k in "oc" for n in "123A" for h in range(2)])

ALU = AluOpType
ACT = ActivationFunctionType


def emit(g, T, ops):
    queue = {"V": g.vector, "A": g.scalar, "T": g.tensor, "G": g, "S": g.sync}
    writer, readers, clock, seq = {}, {}, {q: {} for q in queue}, {q: 0 for q in queue}
    for i, o in enumerate(ops):
        deps = set()
        for k in o["r"]:
            deps.add(writer[k])
        for k in o["w"]:
            if k in writer:
                deps.add(writer[k])
            deps.update(readers.get(k, []))
        deps.discard(i)
        o["waits"] = []
        if o["q"] is None:
            o["knows"] = {}
        else:
            known = clock[o["q"]]
            for d in sorted(deps, reverse=True):
                p = ops[d]
                if known.get(p["lane"], -1) >= p["pos"]:
                    continue
                if p["q"] == "T" and o["q"] == "T":
                    continue
                o["waits"].append(d)
                p["signal"] = True
                for lane, pos in p["knows"].items():
                    known[lane] = max(known.get(lane, -1), pos)
            o["knows"] = dict(known)
        if o["sem"] is None:
            o["lane"], o["pos"] = o["q"], seq[o["q"]]
            seq[o["q"]] += 1
        else:
            o["lane"], o["pos"] = ("dma", i), 0
        o["knows"][o["lane"]] = o["pos"]
        for k in o["r"]:
            readers.setdefault(k, []).append(i)
        for k in o["w"]:
            writer[k] = i
            readers[k] = []
    count = {}
    for o in ops:
        if o["sem"] is not None:
            count[o["sem"]] = count.get(o["sem"], 0) + o["inc"]
            o["at"] = (o["sem"], count[o["sem"]])
        elif o.get("signal"):
            name = "c" + o["q"]
            count[name] = count.get(name, 0) + 1
            o["at"] = (name, count[name])
    for o in ops:
        if o["q"] is None:
            continue
        for d in o["waits"]:
            queue[o["q"]].wait_ge(T.sem[ops[d]["at"][0]], ops[d]["at"][1])
        call = o["fn"]()
        if o["sem"] is None:
            if o.get("signal"):
                call.then_inc(T.sem[o["at"][0]], 1)
        elif o["local"]:
            call.then_inc(T.sem[o["sem"]], 16)
    return count


def rank_program(g, core, T, topo):
    rank = T.rank_of(core)
    if rank is None:
        return
    ops = []
    V, S, PE = g.vector, g.scalar, g.tensor

    def op(q, fn, r, w):
        ops.append({"q": q, "fn": fn, "r": list(r), "w": list(w), "sem": None})

    def dma(q, sem, out, in_, r, w):
        eng = {"A": g.scalar, "S": g.sync, "G": g}[q]
        ops.append({"q": q, "fn": lambda: eng.dma_start(out, in_), "r": list(r), "w": list(w), "sem": sem, "inc": 16, "local": True})

    def ts(out, in0, s1, s2, op0, op1, r, w):
        if op1 is None:
            op("V", lambda: V.tensor_scalar(out, in0, s1, None, op0), r, w)
        else:
            op("V", lambda: V.tensor_scalar(out, in0, s1, s2, op0, op1), r, w)

    def tt(out, in0, in1, alu, r, w):
        op("V", lambda: V.tensor_tensor(out, in0, in1, alu), r, w)

    def cp(out, in_, r, w):
        op("V", lambda: V.tensor_copy(out, in_), r, w)

    def fill(ap, c, w):
        op("V", lambda: V.memset(ap, c), [], w)

    def scan(out, d0, d1, init, op0, op1, r, w):
        op("V", lambda: V.tensor_tensor_scan(out, d0, d1, init, op0, op1), r, w)

    def quant(q, s, t, r, w):
        op("V", lambda: V.quantize_mx(q, s, t), r, w)

    def turn(out, in_, r, w):
        op("V", lambda: V.transpose(out, in_), r, w)

    def act(out, in_, func, r, w, **kw):
        op("A", lambda: S.activation(out, in_, func, **kw), r, w)

    def acp(out, in_, r, w):
        act(out, in_, ACT.Copy, r, w)

    def aff(out, in_, scale, bias, r, w):
        act(out, in_, ACT.Identity, r, w, scale=scale, bias=bias)

    def afill(out, c, w):
        aff(out, T.ones[:, 0:out.shape[1]], 0.0, float(c), ["ones"], w)

    def mm(bank, n, lq, lp, rq, rp, r):
        op("T", lambda: PE.matmul_mx(T["ps%d" % bank][:, 0:n], lq, lp, rq, rp, True, True), r, ["ps%d" % bank])

    def iota(out, pattern, base, cm, w, whole=False):
        if whole:
            op("G", lambda: g.iota(out, pattern, base, cm), [], w)
        else:
            op("G", lambda: g.iota(out, pattern, base, cm, allow_small_or_imprecise_dtypes=True), [], w)

    quarters = lambda k: [k + str(q) for q in range(4)]
    LM, LB, LA, LD = 0, 24, 54, 84
    la = lambda t: T.lu[:, LA + 10 * t:LA + 10 * t + 10]
    lb = lambda t: T.lu[:, LB + 10 * t:LB + 10 * t + 10]
    M0, p0, ramp = T.M0[:], T.pi[:, 0:1], T.true[:, 0:C]
    tcol, qcol, run, half, lane, row = (T.pf[:, i:i + 1] for i in (1, 2, 3, 4, 5, 6))
    file_keys = lambda t: ["x"] + ["F%d%d" % (s, b) for s in range(t) for b in range(4)]
    window = lambda t: T.F[:, 0:4 * (C + A * t)]
    base = lambda t: float(C + A * t - 1)

    dma("S", "dm", T.lst[:, LM:LM + 24], T.m[:], [], ["m"])
    dma("A", "dlb", T.lst[:, LB:LB + 30], T.lb[:], [], ["lb"])
    dma("S", "dla", T.lst[:, LA:LA + 30], T.la[:], [], ["la"])
    dma("S", "dx", T.F[:, 0:4 * C], T.x[:], [], ["x"])
    dma("A", "dld", T.lst[:, LD:LD + 30], T.ld[:], [], ["ld"])
    dma("S", "du", T.ut[:], T.u[:], ["m"], ["ut"])
    dma("S", "dws", T.wp[:], T.ws[:], [], ["wp"])
    dma("S", "dwc", T.wq[:].bitcast(dt.uint8), T.wc[:], [], ["wq"])

    iota(p0, [[0, 1]], 0, 1, ["pi0"], True)
    fill(T.ones[:], 1.0, ["ones"])
    iota(T.em[:], [[0, 40], [512, 4]], 0, 0, ["em"])
    op("G", lambda: g.affine_select(T.eb[:, 0:516], T.ones[:, 0:516], [[-1, 516]], ALU.is_equal, 0.0, 3, 4), ["ones"], ["eb"])
    iota(T.u2i[:], [[2, 4], [0, 2]], 0, 1, ["u2i"], True)
    iota(T.pp[:], [[1, 16], [16, 10]], 1, 0, ["pp"])
    iota(T.DD[:], [[0, 680]], 0, 0, ["DD"])
    scan(ramp, T.ones[:, 0:C], T.ones[:, 0:C], -1.0, ALU.mult, ALU.add, ["ones"], ["ramp"])
    ts(T.pi[:, 1:2], p0, 3, None, ALU.bitwise_and, None, ["pi0"], ["pi1"])
    ts(T.pi[:, 2:3], p0, 2, 3, ALU.logical_shift_right, ALU.bitwise_and, ["pi0"], ["pi2"])
    cp(T.pf[:, 1:3], T.pi[:, 1:3], ["pi1", "pi2"], ["pf"])
    for i in range(2):
        afill(T.inv[:, C * i:C * i + C], 0, ["inv%d" % i])

    def engine_sets(t, src, dst):
        e = topo.engines(src, dst)
        return (e[:len(e) // 2], e[len(e) // 2:]) if t == 0 else (e, e)

    def send(t):
        quant(T["zq%d" % t][:], T["zp%d" % t][:], T.Z[:], ["Z%d" % i for i in range(5)], ["zq%d" % t])
        peer = T.cores[rank ^ STEP[t]]
        rid, pid = topo.addr(peer)[0:2]
        sides = ((T["gq%d" % t][:].bitcast(dt.uint8), T["zq%d" % t][:].bitcast(dt.uint8)), (T["gp%d" % t][:], T["zp%d" % t][:]))
        for (out, in_), es in zip(sides, engine_sets(t, core, peer)):
            mask = sum(1 << e for e in es)
            ops.append({"q": "G", "r": ["zq%d" % t], "w": [], "sem": "sent", "inc": len(es), "local": False,
                        "fn": lambda out=out, in_=in_, mask=mask: g.remote_dma(out, in_, T.sem["arr%d" % t], T.sem.sent, pid, rid, mask)})
        ops.append({"q": None, "r": [], "w": ["gq%d" % t], "sem": "arr%d" % t, "inc": sum(len(es) for es in engine_sets(t, peer, core))})

    def operands(t, shadow):
        keys = file_keys(t)
        for e in range(4):
            acp(T.Bt[:, A * e:A * e + A], window(t).indirect(T.O[:, 24 * e:24 * e + 10]), keys + ["O%d" % e],
                ["Bt%d" % e] + (["Bt4"] if e == 3 else []))
        shadow()
        for e in range(4):
            tt(T.Z[:, e:4 * A:4], window(t).indirect(T.O[:, 24 * e + 10:24 * e + 20]), T.Bt[:, A * e:A * e + A],
               ALU.add, keys + ["O%d" % e, "Bt%d" % e], ["Z%d" % e] + (["Z4"] if e == 3 else []))

    def deal(name, src, n, r):
        for h in range(2):
            dma("S", "dc%s%d" % (name, h), T["crs" + name][:, n * h:n * h + n], src[16 * h:128:32, :], r, ["crs%s%d" % (name, h)])
        for h in range(2):
            dma("S", "do%s%d" % (name, h), T["own" + name][:, n * h:n * h + n], src[0:128:16, 16 * n * h:16 * n * (h + 1)], r, ["own%s%d" % (name, h)])

    own = lambda name: ["own%s0" % name, "own%s1" % name]

    def crossed(out, name, n, k, tab, add=0.0):
        for q in range(2):
            ts(T[out][:, q:2 * n:2], T["crs" + name][:, n * k * q + tab:n * k * (q + 1):k], add, None, ALU.add, None,
               ["crs%s%d" % (name, q)], [out + str(q)])

    def lookup(ro, k, tab, win, lists, r, add=0.0):
        for h in range(2):
            aff(T[ro][:, A * k * h + tab:A * k * (h + 1):k], win.indirect(lists[h]), 1.0, add, r, ["%s%d%d" % (ro, tab, h)])

    AT = {"D0": 0, "D1": 120, "D3": 240, "D0p": 360, "D0q": 480, "cm": 600, "b1": 648}
    D = lambda d, a, b, s=1: T.DD[:, AT[d] + a:AT[d] + b:s]
    keep = lambda t: T.k8[:, 8:9] if t == 2 else D("D%d" % t, 26, 27)
    signs = lambda t: T.sg[:, 176 * t:176 * t + A + 1]

    def choose(out, d0, d1, n, turned, r, w, alu=ALU.max):
        x = 0 if n == 20 else 2
        cp(D(d0, 25, 120, 3), T[turned][:, 0:16 * n].indirect(T.XL[:, x:x + 2]), r + ["XL%d" % x, "XL%d" % (x + 1), "DD"], [d0 + "e"])
        scan(T[out][:, 0:3 * n], D(d0, 24, 24 + 3 * n), T[d1][:, 0:3 * n], 0.0, ALU.mult, alu,
             ["DD", d0 + "e", d0 + "k"] + (own("1") if d1 == "own1" else [d1 + "a", d1 + "b", d1 + "c"]), w)

    def keep_in(d0, t, n):
        ts(D(d0, 26, 26 + 3 * n, 3), T.ones[:, 0:n], keep(t), 0.0, ALU.mult, ALU.max, ["ones", "DD", "D%dk" % t], [d0 + "k"])

    def after_arrival(t, v1):
        gq, gp, n = T["gq%d" % t][:], T["gp%d" % t][:], (24 if t == R - 1 else 20)
        KX, win = T["KX%d" % t], signs(t)
        for b in range(4):
            mm(b, A, T.wq[:, 128 * b:128 * b + 128], T.wp[:, 128 * b:128 * b + 128], gq, gp, ["wq", "wp", "gq%d" % t])
        for b in range(4):
            bank = T["ps%d" % b][:, 0:A]
            if b % 2 == 1:
                ts(T.H[:, b:4 * A:4], bank, 0.0, 0.015625, ALU.max, ALU.mult, [], ["H%d" % b, "ps%d" % b])
            else:
                act(T.H[:, b:4 * A:4], bank, ACT.Relu, [], ["H%d" % b, "ps%d" % b], scale=0.015625)
        quant(T.hq[:], T.hp[:], T.H[:], quarters("H"), ["hq"])
        v1()
        mm(5, A, T.u2q[:], T.u2p[:], T.hq[:], T.hp[:], ["u2q", "u2p", "hq"])
        for b in range(4):
            mm(b, A, T.eq[:, 128 * b:128 * b + 128], T.ep[:, 128 * b:128 * b + 128], T.hq[:], T.hp[:], ["eq%d" % b, "hq"])
        act(T.sg[:, 176 * t + 1:176 * t + A + 1], T.ps5[:, 0:A], ACT.Sign, [], ["key", "sg%d" % t, "ps5"],
            scale=2.0 ** 32, bias=2.0 ** -120, accum_out=T.key[:, 0:1])
        keys = ["sg%d" % t, "sgc", "KX%d0" % t, "KX%d1" % t]
        c = 6
        acp(T.Rc[:, 16 * c:16 * n], win.indirect(KX[:, c:n]), keys, ["Rc1"])
        lo = 4 * (C + A * t)
        for b in range(4):
            acp(T.F[:, lo + b:lo + 4 * A:4], T["ps%d" % b][:, 0:A], [], ["F%d%d" % (t, b), "ps%d" % b])
        scan(T.bc[:], T.b0[:], D("b1", 0, 32), T.key[:, 0:1], ALU.mult, ALU.add, ["b0", "b0a", "b0b", "b1", "key"], ["bc"])
        cp(T.Rc[:, 0:16 * c], win.indirect(KX[:, 0:c]), keys, ["Rc0"])
        turn(T.tr[:], T.bc[:], ["bc"], ["tr"])
        turn(T.Tc[:, 0:16 * c], T.Rc[:, 0:16 * c], ["Rc0"], ["Tc0"])
        ts(D("cm", 0, 8), T.tr[:, 0:8], T.tr[:, 8:9], T.tr[:, 9:10], ALU.subtract, ALU.is_gt, ["tr", "DD"], ["cm"])
        turn(T.Tc[:, 16 * c:16 * n], T.Rc[:, 16 * c:16 * n], ["Rc1"], ["Tc1"])
        last = t == R - 1
        m = 9 if last else 28
        scan(T.k8[:, 0:m] if last else D("D%d" % t, 2, 3 * m, 3), D("cm", 0, m), T.ones[:, 0:m], -1.0, ALU.add, ALU.min,
             ["cm", "DD", "ones"], ["D%dk" % t])
        if last:
            keep_in("D3", t, n)
            choose("Xc", "D3", "D21", n, "Tc", ["Tc0", "Tc1"], ["Xc"], ALU.add)
        else:
            choose("Xc", "D%d" % t, ("own1", "D11")[t], n, "Tc", ["Tc0", "Tc1"], ["Xc"])
        for e in ((0, 2, 1, 3) if last else range(4)):
            ts(T.O[:, 24 * e:24 * e + n], T.Xc[:, 2:3 * n:3], 2.0 if last else 4.0, float(e), ALU.mult, ALU.add, ["Xc"], ["O%d" % e])

    MK = ["M0a", "M0b"]
    L90, n90 = T.lst[:, LB:LB + 90], ["la", "lb", "ld"]
    cp(T.lu[:, LM:LM + 24], T.lst[:, LM:LM + 24], ["m"], ["mu"])
    ts(T.mask4[:], T.em[:], 1.0 / 512, qcol, ALU.mult, ALU.is_equal, ["em", "pf"], ["mask4"])
    ts(T.pi[:, 4:5], p0, 4, 1, ALU.logical_shift_right, ALU.bitwise_and, ["pi0"], ["pi4"])
    acp(T.M0[:, 192:C], ramp.indirect(T.lu[:, 12:24]), ["ramp", "mu"], ["M0b"])
    afill(T.inv[:, 2 * C:3 * C], 0, ["inv2"])
    afill(T.b0[:], 1, ["b0", "b0a", "b0b"])
    afill(T.sg[:, 0:R * 176:176], -1, ["sgc"])
    cp(T.M0[:, 0:192], ramp.indirect(T.lu[:, 0:12]), ["ramp", "mu"], ["M0a"])
    cp(T.lu[:, LB:LD], T.lst[:, LB:LD], ["la", "lb"], ["lu"])
    ts(T.pi[:, 5:6], p0, 15, None, ALU.bitwise_and, None, ["pi0"], ["pi5"])
    tt(T.Pn[:, 0:A], M0.indirect(lb(0)), T.mask4[:], ALU.mult, MK + ["lu", "mask4"], ["Pn0"])
    tt(T.Pn[:, A:2 * A], M0.indirect(la(0)), T.mask4[:], ALU.mult, MK + ["lu", "mask4"], ["Pn1"])
    scan(T.Xn[:, 0:A], T.em[:], T.Pn[:, 0:A], 0.0, ALU.min, ALU.max, ["em", "Pn0"], ["Xn0"])
    ts(T.ln[:, 0:90], L90, 31, None, ALU.bitwise_and, None, n90, ["ln"])
    ts(T.O0[:, 0:40], T.Xn[:, 3:A:4], 4.0, tcol, ALU.mult, ALU.add, ["Xn0", "pf"], ["O00"])
    scan(T.Xn[:, A:2 * A], T.em[:], T.Pn[:, A:2 * A], 0.0, ALU.min, ALU.max, ["em", "Pn1"], ["Xn1"])
    ts(T.rb[:, 0:90], T.ln[:, 0:90], 383.0, None, ALU.mult, None, ["ln"], ["rb"])
    ts(T.O0[:, 40:80], T.Xn[:, A + 3:2 * A:4], 4.0, tcol, ALU.mult, ALU.add, ["Xn1", "pf"], ["O01"])
    ts(T.pi[:, 6:7], p0, 4, 6, ALU.logical_shift_right, ALU.bitwise_and, ["pi0"], ["pi6"])
    ts(T.pi[:, 3:4], p0, 31, None, ALU.bitwise_and, None, ["pi0"], ["pi3"])
    cuts = [0, 6, 16, 26, 34, 40]
    for i in range(5):
        a, b = cuts[i], cuts[i + 1]
        acp(T.Bt[:, 16 * a:16 * b], window(0).indirect(T.O0[:, a:b]), ["x", "O00"], ["Bt%d" % i])
    for i in range(5):
        a, b = cuts[i], cuts[i + 1]
        tt(T.Z[:, 16 * a:16 * b], window(0).indirect(T.O0[:, 40 + a:40 + b]), T.Bt[:, 16 * a:16 * b], ALU.add, ["x", "O01", "Bt%d" % i], ["Z%d" % i])
    send(0)

    iota(T.true[:, C:C + A], [[1, A]], C, 0, ["true0"])
    iota(T.true[:, C + A:C + 3 * A], [[A, 2], [1, 10], [10, 16]], C + A, 0, ["true1"])
    lookup("ro1", 3, 1, M0, (lb(1), la(1)), MK + ["lu"])
    lookup("ro1", 3, 2, M0, (lb(1), la(1)), MK + ["lu"])
    lookup("ro2", 2, 1, M0, (lb(2), la(2)), MK + ["lu"])
    tt(T.ra[:, 0:90], T.rb[:, 0:90], L90, ALU.add, ["rb"] + n90, ["ra"])
    tt(T.pi[:, 7:8], p0, T.pi[:, 6:7], ALU.add, ["pi0", "pi6"], ["pi7"])
    ts(T.k0[:, 0:70], T.ra[:, 0:70], 3.0 / 32, None, ALU.mult, None, ["ra"], ["k0"])
    ts(T.u2j[:], T.u2i[:], 7, None, ALU.bitwise_and, None, ["u2i"], ["u2j"])
    cp(T.inv[:].indirect(T.k0[:, 60:70]), T.true[:, 1:A + 1], ["ramp", "k0"], ["inv", "inv0", "inv1", "inv2"])
    ts(T.pi[:, 6:7], T.pi[:, 7:8], 7, None, ALU.bitwise_and, None, ["pi7"], ["pi6"])
    ts(T.UL[:], T.u2j[:], 16.0, None, ALU.mult, None, ["u2j"], ["UL"])
    quant(T.uq[:], T.up[:], T.ut[:], ["ut"], ["uq"])
    cp(T.pf[:, 3:7], T.pi[:, 3:7], ["pi3", "pi4", "pi5", "pi6"], ["pf2"])
    cp(T.u2q[:].bitcast(dt.uint32), T.uq[:].bitcast(dt.uint32).indirect(T.UL[:]), ["uq", "UL"], ["u2q"])
    ts(T.cf[:, 5:6], run, 9.0, 4095.0, ALU.is_equal, ALU.mult, ["pf2"], ["cf5"])
    lookup("ro1", 3, 0, T.inv[:], (T.k0[:, 10:20], T.k0[:, 40:50]), ["inv", "k0"], base(0))
    deal("1", T.ro1, 30, ["ro1%d%d" % (k, h) for k in range(3) for h in range(2)])
    aff(T.cf[:, 4:5], row, -0.125, A / 2 + 0.875, ["pf2"], ["cf4"])
    aff(T.cf[:, 0:1], lane, 32.0, half, ["pf2"], ["cf0"])
    acp(T.u2p[:], T.up[:].indirect(T.UL[:]), ["uq", "UL"], ["u2p"])
    lookup("ro2", 2, 0, T.inv[:], (T.k0[:, 20:30], T.k0[:, 50:60]), ["inv", "k0"], base(0))
    deal("2", T.ro2, 20, ["ro2%d%d" % (k, h) for k in range(2) for h in range(2)])
    ts(T.b0[:, 16:17], run, 8.0, T.cf[:, 5:6], ALU.not_equal, ALU.add, ["pf2", "cf5"], ["b0b"])
    ts(T.b0[:, 0:1], T.cf[:, 5:6], -4096.0, 1.0 / 8192, ALU.add, ALU.mult, ["cf5"], ["b0a"])
    ts(T.cf[:, 1:2], lane, 10.0, -304.0, ALU.is_ge, ALU.mult, ["pf2"], ["cf1"])
    for b in range(4):
        quant(T.eq[:, 128 * b:128 * b + 128], T.ep[:, 128 * b:128 * b + 128], T.eb[:, 3 - b:515 - b], ["eb"], ["eq%d" % b])
    ts(D("b1", 0, 1), T.cf[:, 4:5], T.b0[:, 0:1], -2.0, ALU.mult, ALU.mult, ["cf4", "b0a", "DD"], ["b1"])
    ts(T.k1[:, 0:90], T.ra[:, 0:90], 3.0 / 32, 1.0, ALU.mult, ALU.add, ["ra"], ["k1"])
    ts(T.XL[:, 0:1], T.cf[:, 0:1], T.cf[:, 1:2], None, ALU.add, None, ["cf0", "cf1"], ["XL0"])
    ts(T.XL[:, 1:2], T.cf[:, 0:1], 208.0, 319.0, ALU.add, ALU.min, ["cf0"], ["XL1"])
    dma("S", "dv", T.vt[:], T.v[:], ["gq0"], ["vt"])

    def gap0():
        crossed("KX0", "1", 10, 3, 0, -base(0))
        cp(T.inv[:].indirect(T.k1[:, 70:80]), T.pp[:], ["pp", "k1"], ["inv"])
    after_arrival(0, gap0)
    operands(1, lambda: crossed("KP0", "2", 10, 2, 0, -base(0)))
    send(1)

    lookup("ro3", 1, 0, T.inv[:], (T.k1[:, 20:30], T.k1[:, 50:60]), ["inv", "k1"], base(1))
    acp(T.Rp[:, 0:2 * A], signs(0).indirect(T.KP0[:, 0:20]), ["sg0", "sgc", "KP00", "KP01"], ["Rp"])
    ts(T.k2[:, 0:10], T.ra[:, 80:90], 3.0 / 32, 2.0, ALU.mult, ALU.add, ["ra"], ["k2"])
    cp(T.inv[:].indirect(T.k2[:, 0:10]), T.pp[:], ["pp", "k2"], ["inv"])
    deal("3", T.ro3, 10, ["ro300", "ro301", "inv"])
    deal("A", T.inv, 36, ["inv"])
    turn(T.Tp[:, 0:2 * A], T.Rp[:, 0:2 * A], ["Rp"], ["Tp"])
    quant(T.vq[:], T.vp[:], T.vt[:], ["vt"], ["vq"])
    acp(T.Dp[:, 0:60:3], T.own2[:, 0:40:2], own("2"), ["Dpa"])
    acp(T.Dp[:, 1:60:3], T.own2[:, 1:40:2], own("2"), ["Dpb"])
    acp(T.Dp[:, 2:60:3], T.own2[:, 1:40:2], own("2"), ["Dpc"])
    aff(T.cf[:, 2:3], lane, 16.0, half, ["pf2"], ["cf2"])
    acp(T.D11[:, 2:60:3], T.own2[:, 1:40:2], own("2"), ["D11c"])
    choose("Xp", "D0", "Dp", 20, "Tp", ["Tp"], ["Xp"])
    cp(T.XL[:, 2:3], T.cf[:, 2:3], ["cf2"], ["XL2"])
    ts(T.XL[:, 3:4], T.cf[:, 2:3], 256.0, 383.0, ALU.add, ALU.min, ["cf2"], ["XL3"])
    acp(T.D11[:, 1:60:3], T.Xp[:, 2:60:3], ["Xp"], ["D11b"])

    def gap1():
        crossed("KX1", "3", 10, 1, 0, -base(1))
        cp(T.D11[:, 0:60:3], T.own3[:], own("3"), ["D11a"])
    after_arrival(1, gap1)
    operands(2, lambda: crossed("KP1", "A", 12, 3, 0))
    send(2)

    crossed("KP2", "A", 12, 3, 1)
    crossed("KX2", "A", 12, 3, 2)
    acp(T.Rp[:], signs(0).indirect(T.KP1[:]), ["sg0", "sgc", "KP10", "KP11"], ["Rp"])
    acp(T.Rq[:], signs(1).indirect(T.KP2[:]), ["sg1", "sgc", "KP20", "KP21"], ["Rq"])
    m24 = T.lst[:, LM:LM + 24]
    for h in range(2):
        ts(T.Dp[:, 3 * h:72:6], T.ownA[:, 36 * h:36 * h + 36:3], base(0), None, ALU.add, None, own("A"), ["Dpa" + "+" * h])
    cp(T.Dp[:, 1:72:3], m24, ["m"], ["Dpb"])
    cp(T.Dp[:, 2:72:3], m24, ["m"], ["Dpc"])
    turn(T.Tp[:], T.Rp[:], ["Rp"], ["Tp"])
    keep_in("D0p", 0, 24)
    for h in range(2):
        ts(T.Dq[:, 3 * h:72:6], T.ownA[:, 36 * h + 1:36 * h + 36:3], base(1), None, ALU.add, None, own("A"), ["Dqa" + "+" * h])
    choose("Xp", "D0p", "Dp", 24, "Tp", ["Tp", "Dpa+"], ["Xp"])
    turn(T.Tq[:], T.Rq[:], ["Rq"], ["Tq"])
    keep_in("D0q", 1, 24)
    cp(T.Dq[:, 2:72:3], m24, ["m"], ["Dqc"])
    acp(T.Dq[:, 1:72:3], T.Xp[:, 2:72:3], ["Xp"], ["Dqb"])
    aff(T.D21[:, 2:72:3], T.Xp[:, 2:72:3], 2.0, 0.0, ["Xp"], ["D21c"])
    for h in range(2):
        aff(T.w1[:, h:24:2], T.ownA[:, 36 * h + 2:36 * h + 36:3], 1.0, base(2), own("A"), ["w1" + "+" * h])
    choose("Xq", "D0q", "Dq", 24, "Tq", ["Tq", "Dqa+"], ["Xq"])

    def gap2():
        tt(T.w2[:], T.w1[:], T.D21[:, 2:72:3], ALU.subtract, ["w1", "w1+", "D21c"], ["w2"])
        tt(T.D21[:, 0:72:3], T.w1[:], T.Xq[:, 2:72:3], ALU.subtract, ["w1", "w1+", "Xq"], ["D21a"])
        tt(T.D21[:, 1:72:3], T.w2[:], T.Xq[:, 2:72:3], ALU.add, ["w2", "Xq"], ["D21b"])
    after_arrival(2, gap2)

    keys = file_keys(R)

    def gather(q, e, a, b):
        (acp if q == "A" else cp)(T.Tt[:, 64 * a + e:64 * b:4], window(R).indirect(T.O[:, 24 * e + a:24 * e + b]), keys + ["O%d" % e], ["T%d%d" % (e, a)])

    def piece(i, a, b, r):
        quant(T.tq[:, a:b], T.tp[:, a:b], T.Tt[:, 4 * a:4 * b], r, ["tq%d" % i])
        mm(5 + i, b - a, T.vq[:], T.vp[:], T.tq[:, a:b], T.tp[:, a:b], ["vq", "tq%d" % i])
        dma("S", "outs", T.oc[:, 4 * a:4 * b], T.tq[:, a:b].bitcast(dt.uint8), ["tq%d" % i], [])

    def y_out(i, a, b):
        bank = "ps%d" % (5 + i)
        cp(T.ys[:, a:b], T[bank][:, 0:b - a], [], ["ys%d" % i, bank])
        dma("S", "outs", T.y[:, a:b], T.ys[:, a:b], ["ys%d" % i], [])
    gather("A", 0, 0, 16)
    ts(T.O[:, 96:120], T.Xc[:, 2:72:3], 0.5, None, ALU.mult, None, ["Xc"], ["O4"])
    gather("V", 1, 0, 16)
    gather("A", 2, 0, 16)
    gather("V", 3, 0, 16)
    for e in range(3):
        gather("A", e, 16, 24)
    piece(0, 0, 256, ["T%d0" % e for e in range(4)])
    gather("V", 3, 16, 24)
    piece(1, 256, C, ["T%d16" % e for e in range(4)])
    acp(T.omr[:], T.true[:].indirect(T.O[:, 96:120]), ["ramp", "true0", "true1", "O4"], ["omr"])
    dma("A", "outs", T.om[:], T.omr[0:128:16, :], ["omr"], [])
    y_out(0, 0, 256)
    y_out(1, 256, C)
    for k in range(4):
        dma("A", "outs", T.osc[4 * k:4 * k + 4, :], T.tp[32 * k:32 * k + 4, :], ["tq0", "tq1"], [])

    count = emit(g, T, ops)
    g.wait_ge(T.sem.sent, count["sent"])
    g.wait_ge(T.sem.outs, count["outs"])
